import numpy as np, ml_dtypes
CORES = [2,6,10,14,18,22,26,30]
N = 8
import mx_ref
BF = ml_dtypes.bfloat16
def gcols(t, e):
    v = np.concatenate([t.reshape(8, 16, -1, 4), np.zeros((8, 16, 1, 4), BF)], axis=2)
    return np.ascontiguousarray(np.stack([v[g][:, e[g]] for g in range(8)])).reshape(128, -1)
def tile(rs):
    return np.stack(rs, axis=2).reshape(128, -1).astype(BF)
def cut(t, i, w=512):
    return t[:, w * i:w * i + w]
def pick(q, e):
    c = np.concatenate([q[0].reshape(128, -1, 4), np.zeros((128, 1, 4), np.uint8)], axis=1); s = np.concatenate([q[1], np.ones((16, 1), np.uint8)], axis=1)
    return (np.ascontiguousarray(c[:, e].reshape(128, -1)), np.ascontiguousarray(s[:, e]))
def join(*qs):
    return (np.concatenate([q[0] for q in qs], axis=1), np.concatenate([q[1] for q in qs], axis=1))
def put(q, e, v):
    c, s = q[0].reshape(128, -1, 4).copy(), q[1].copy(); c[:, e] = v[0].reshape(128, -1, 4); s[:, e] = v[1]
    return (c.reshape(128, -1), s)
def pk(c, s):
    return (np.ascontiguousarray(c), mx_ref.live(s))
def emit(q):
    return q[0], q[1]
def packed(v, rng):
    q = [mx_ref.quantize(np.ascontiguousarray(v[r])) for r in range(N)]
    return np.stack([a for a, b in q]), np.stack([mx_ref.plane(b, rng) for a, b in q])
def values_of_codes():
    e, c = np.zeros((128, 128, 4), np.float32), np.zeros((128, 2, 4), np.uint8)
    e[np.arange(128), np.arange(128), 0] = 1
    c[:127, :, 0] = np.arange(256).reshape(2, 128).T[:127]
    return mx_ref.matmul(mx_ref.quantize(e.reshape(128, 512).astype(BF)), (c.reshape(128, 8), np.full((16, 2), 127, np.uint8))).T.reshape(-1).astype(np.float64)
CODE_VALUE, SCALE_VALUE = values_of_codes(), 2.0 ** (np.arange(256) - 127.0)
def decode(q):
    return (CODE_VALUE[q[0]].reshape(16, 8, -1, 4) * SCALE_VALUE[q[1]][:, None, :, None] + 0.0).reshape(128, -1).astype(np.float32)
def f(rng, *shape):
    return mx_ref.flush((rng.standard_normal(shape, dtype=np.float32) * np.exp2(rng.integers(-2, 3, shape[:-1] + (1,)))).astype(BF))
def wide(rng, *shape, cols=0):
    v = rng.standard_normal(shape, dtype=np.float32) * np.exp2(rng.integers(-12, 13, shape)).astype(np.float32)
    if cols: v *= np.repeat(np.exp2(rng.integers(-cols, cols + 1, shape[:-2] + (1, shape[-1] // 4))) * (rng.random(shape[:-2] + (1, shape[-1] // 4)) > 0.0625), 4, axis=-1).astype(np.float32)
    return mx_ref.flush(v.astype(BF))
C, B, F, K, R = 512, 10, 2, 2, 2
T = 2 ** B
def keys(p):
    m = (p.reshape(8, 16, C) < 0).astype(np.int64)
    return np.sum(m[:, :B] << np.arange(B)[:, None], axis=1), np.sum(m[:, B:B + F] << np.arange(F)[:, None], axis=1)
def insert(a):
    slots, free = np.full((8, T), -1), np.ones((8, C), bool)
    for k in range(K):
        for g in range(8):
            s = (a[g] + k) % T
            want = np.flatnonzero(free[g] & (slots[g][s] < 0))
            at, first = np.unique(s[want], return_index=True)
            slots[g, at] = want[first]
            free[g, want[first]] = False
    return slots
def search(slots, held, a, h):
    found = np.full((8, C), -1)
    for k in range(K):
        c = np.take_along_axis(slots, (a + k) % T, axis=1)
        hit = (found < 0) & (c >= 0) & (np.take_along_axis(held, np.maximum(c, 0), axis=1) == h)
        found[hit] = c[hit]
    return found
def numbers_of(rng):
    return {"x": np.array(f(rng, N, 128, 4 * C)), "u": np.array(f(rng, N, 128, 512)), "v": np.array(f(rng, N, 128, 512))}
def weights(rng, w):
    c, p = packed(w, rng)
    return {"wc": c, "ws": p}
def still(rng):
    w = np.zeros((N, 128, 4, 128, 4), np.float32)
    i = np.arange(128)
    for b in range(4): w[:, i, b, i, b] = 32
    return weights(rng, w.reshape(N, 128, 2048).astype(BF))
def spots(rng):
    e = np.stack([np.concatenate([[0, T - 1], 1 + rng.permutation(T - 2)[:C - 2]]) for g in range(8)])
    return rng.permuted(np.tile(e, (N, 1, 1)), axis=2)
def plant(d, rng, a, h, size, look):
    x, u = d["x"].reshape(N, 8, 16, C, 4), d["u"].reshape(N, 128, 8, 16, 4)
    k = ((a + (h << B))[..., None] >> np.arange(16)) & 1
    m = np.where(k == 1, -1.0, rng.integers(0, 2, k.shape)) * size[:, None, None, None]
    m[..., B + F:] = 0
    x[:, :, :8] = 0
    x[:, :, :4] = m.reshape(N, 8, C, 4, 4).transpose(0, 1, 3, 2, 4).astype(np.float32).astype(BF)
    u[:, :, :, :B + F] = 0
    for g in range(8):
        for i in range(B + F): u[:, 16 * g + i // 4, g, i, i % 4] = look.astype(np.float32).astype(BF)
    return {"x": x.reshape(N, 128, 4 * C), "u": u.reshape(N, 128, 512), "v": d["v"], **still(rng)}
def setup_inputs(rng):
    return {**numbers_of(rng), **weights(rng, f(rng, N, 128, 2048))}
def setup_inputs_crowd(rng):
    s = T - C // 4 - 4
    a = (s + np.repeat(np.arange(C // 2), np.tile([3, 1, 0, 4, 0, 0, 6, 2], C // 16))) % T
    a = rng.permuted(np.tile(a, (N, 8, 1)), axis=2)
    e = int(rng.integers(N))
    o = rng.permutation(8)
    m = np.where(o % 2 == 0, C // 32, rng.integers(0, C // 16, 8))
    z = (s + 3 + 8 * ((m + 1 + rng.integers(0, C // 16 - 1, 8)) % (C // 16))) % T
    a[e] = ((s + 3 + 8 * m) % T)[:, None]
    h = rng.integers(0, 2 ** F, (N, 8, C))
    b, n = (e - 1) % N, (e + 1) % N
    for g in range(8):
        if o[g] < 4:
            a[e, g, C - K:] = z[g]
            h[e, g, C - K:] = rng.permutation(2 ** F)[:K]
            j = np.flatnonzero(a[b, g] == z[g])[0]
            a[b, g, j] = a[b, g, C - 1]
            a[b, g, C - 1] = z[g]
            h[b, g, a[b, g] == z[g]] = h[e, g, C - 1]
        else:
            h[e, g, K:] = h[n, g, np.flatnonzero(a[n, g] == a[e, g, 0])[0]]
    size = np.where((np.arange(N) + rng.integers(2)) % 2 == 0, 64.0, 1.0)
    return plant(numbers_of(rng), rng, a, h, size, np.ones(N))
def setup_inputs_found(rng):
    e = int(rng.integers(N))
    a = spots(rng)
    z, c = (e + 2) % N, int(rng.integers(1, C))
    for g in range(8):
        a[z, g, np.flatnonzero(a[z, g] == 0)[0]] = a[z, g, c]
        a[z, g, c] = 0
    h = np.tile(rng.integers(0, 2 ** F, (8, 1)) * (rng.permutation(8) % 2)[:, None], (N, 1, C))
    h[e] = (h[e] + 1) % 2 ** F
    d = plant(numbers_of(rng), rng, a, h, np.ones(N), np.ones(N))
    x = d["x"].reshape(N, 128, C, 4)
    x[z, :, c] = 0
    return {**d, "x": x.reshape(N, 128, 4 * C)}
def setup_inputs_sizes(rng):
    small = (np.arange(N) + rng.integers(N)) % N < N // 2
    a = spots(rng)
    h = rng.integers(0, 2 ** F, (N, 8, C))
    return plant(numbers_of(rng), rng, a, h, np.where(small, 2.0 ** -30, 2.0 ** 27), np.where(small, 2.0 ** -30, 2.0 ** 30))
def setup_inputs_spread(rng):
    d = setup_inputs(rng)
    d["x"] = wide(rng, N, 128, 4 * C, cols=6)
    return d
def check_inputs(d):
    b = []
    for k in ("x", "u", "v"):
        a = np.abs(d[k].astype(np.float32))
        if not (np.isfinite(a).all() and ((a == 0) | (a >= 2.0 ** -30) & (a <= 2.0 ** 30)).all()): b.append("a value of " + k)
    c, s = d["wc"] & 127, np.stack([mx_ref.live(p) for p in d["ws"]])
    if (c == 127).any(): b.append("a code of wc")
    if ((s < 85) | (s > 160))[c.reshape(N, 16, 8, 512, 4).max(axis=(2, 4)) > 0].any(): b.append("a scale of ws")
    return b
def reference(x, u, v, wc, ws):
    qu = [mx_ref.quantize(u[r]) for r in range(N)]
    lay = [pk(wc[r], ws[r]) for r in range(N)]
    now = [x[r] for r in range(N)]
    for t in range(R):
        made, a, h, slots, answers = [], [], [], [], []
        for r in range(N):
            q = mx_ref.quantize(now[r])
            made.append(tile([mx_ref.matmul(pick(lay[r], np.arange(128 * b, 128 * b + 128)), q) * np.float32(0.03125) for b in range(4)]))
            mx_ref.quantize(made[r])
            i, j = keys(mx_ref.matmul(qu[r], q))
            a.append(i)
            h.append(j)
            slots.append(insert(i))
        for r in range(N):
            n = (r + 1) % N
            answers.append(mx_ref.quantize(gcols(made[n], search(slots[n], h[n], a[r], h[r]))))
        came = decode(join(*answers))
        now = [(made[r].astype(np.float32) + cut(came, r, 4 * C)).astype(BF) for r in range(N)]
    y = np.zeros((N, 128, C), np.float32)
    oc, osc = np.zeros((N, 128, 4 * C), np.uint8), np.zeros((N, 16, C), np.uint8)
    for r in range(N):
        q = mx_ref.quantize(now[r])
        y[r] = mx_ref.matmul(mx_ref.quantize(v[r]), q)
        oc[r], osc[r] = emit(q)
    return {"y": y, "oc": oc, "osc": osc}

@@ -1,0 +1,321 @@
+import numpy as np
+from concourse.bass import DstId, RemoteDMATransfer
+from concourse.mybir import dt, AluOpType as OP, ActivationFunctionType as AF
+
+F32, BF, I32, U16, U8, MX = "float32", "bfloat16", "int32", "uint16", "uint8", "float8_e4m3fn_x4"
+ROUNDS = 2
+LN2 = float(np.log(2.0))
+SCRATCH = {"psR": ("psum", [128, 2048], F32), "psS": ("psum", [128, 512], F32), "psM": ("psum", [128, 512], F32), "psA": ("psum", [128, 1024], F32)}
+for _d, _s in [
+    (BF, "xin 2048 X1 2048 X2 2048 uin 512 vin 512 P 2048 dw 2112 ones 512 me 64 m0 128 cc 3584 ce 2048 mk 1536 rs 1024 bu 2048 bq 512 EA 512 EB 512 hq_0 64 hq_1 64 qh_0 64 qh_1 64"),
+    (MX, "uq 128 vq 128 wq 512 kq 896 eq 512 xq_0 512 xq_1 512 xq_2 512 buq 512 bqq 128 eqa 128 eqb 128 pq_0 512 pq_1 512 lc_0 512 lc_1 512"),
+    (U8, "us 128 vs 128 wsc 512 ks 896 es 512 xs_0 512 xs_1 512 xs_2 512 bus 512 bqs 128 esa 128 esb 128 psc_0 512 psc_1 512 ls_0 512 ls_1 512"),
+    (F32, "yo 512 pF 5 iot 32 w4 128 g8 8 gg 8 gp 8 gm 8 wx 1 wxh 1 tw 4 w8a 8 w8h 8 w8n 8 ba 8 ba0 8 ba1 8 mk4 128 mp 512 idc 512 cs8 32 dc 2 "
+          "AA 512 AB 512 TA 512 TB 512 e1 128 e2 64 aw 32 a1 32 h1 128 h2 64 vv 512 y1 128 y2 64 yw 32 rk 32 tab_0 1056 tab_1 1056 "
+          "FE 1024 SC 1024 FG 1024 SD 1024 s1 32 s3 32 s4 32 s5 32 s6 32 qf 64 r3 64 r4 64"),
+    (I32, "pI 1 pK 5 i1 32 i2 32 r1 64 r2 64 r5 32 r6 32"),
+    (U16, "la_0 64 la_1 64 of1 32 of2 32 ql_0 64 ql_1 64 lo_0 32 lo_1 32 li_0 32 li_1 32"),
+]:
+    _s = _s.split()
+    for _i in range(0, len(_s), 2):
+        SCRATCH[_s[_i]] = ("sbuf", [128, int(_s[_i + 1])], _d)
+SEMAPHORES = ["sv", "sa", "sp", "sg", "ldx0", "ldx1", "ldu", "ldv", "ldw", "ldws", "sty", "stc", "sts", "sent",
+              "gotq0", "gotq1", "gotc0", "gotc1", "gotl0", "gotl1"]
+
+
+def rank_program(g, core, T, topo):
+    me = T.rank_of(core)
+    if me is None:
+        return
+    n = len(T.cores)
+    nxt, prv = T.cores[(me + 1) % n], T.cores[(me - 1) % n]
+    V, S, PE = g.vector, g.scalar, g.tensor
+    queue = {"v": V, "a": S, "p": PE, "g": g, "y": g.sync}
+    own = {"v": "sv", "a": "sa", "p": "sp", "g": "sg"}
+    count = {"sv": 0, "sa": 0, "sp": 0, "sg": 0}
+    seen = {q: {} for q in queue}
+    sent = [0]
+    late = {}
+
+    def need(q, deps):
+        for d in deps:
+            if d is not None and seen[q].get(d[0], 0) < d[1]:
+                queue[q].wait_ge(T.sem[d[0]], d[1])
+                seen[q][d[0]] = d[1]
+
+    def done(q, ins):
+        s = own[q]
+        ins.then_inc(T.sem[s], 1)
+        count[s] += 1
+        return (s, count[s])
+
+    def vec(deps, fn, *a):
+        need("v", deps)
+        return done("v", fn(*a))
+
+    def ts(deps, out, in0, s1, s2, *ops):
+        return vec(deps, V.tensor_scalar, out, in0, s1, s2, *ops)
+
+    def tt(deps, out, in0, in1, op):
+        return vec(deps, V.tensor_tensor, out, in0, in1, op)
+
+    def act(deps, out, in_, func=AF.Copy, **kw):
+        need("a", deps)
+        return done("a", S.activation(out, in_, func, **kw))
+
+    def mm(deps, out, lq, ls, rq, rs, start=True, stop=True):
+        need("p", deps)
+        return done("p", PE.matmul_mx(out, lq, ls, rq, rs, start, stop))
+
+    def iota(out, pattern, base=0, cm=0):
+        return done("g", g.iota(out, pattern, base, cm, allow_small_or_imprecise_dtypes=True))
+
+    def select(deps, out, in_, pattern, op, base=0, cm=0):
+        need("g", deps)
+        return done("g", g.affine_select(out, in_, pattern, op, 0.0, base, cm))
+
+    def load(q, sem, out, in_):
+        queue[q].dma_start(out, in_).then_inc(T.sem[sem], 16)
+        return (sem, 16)
+
+    def bits(es):
+        m = 0
+        for e in es:
+            m |= 1 << e
+        return m
+
+    def remote(deps, dst, out, in_, sem):
+        need("g", deps)
+        rid, pid = topo.addr(dst)[:2]
+        g.remote_dma(out, in_, T.sem[sem], T.sem.sent, pid, rid, topo.mask(core, dst))
+        sent[0] += len(topo.engines(core, dst))
+
+    d_x0 = load("y", "ldx0", T.xin[:, 0:1024], T.x[:, 0:1024])
+    d_u = load("a", "ldu", T.uin[:], T.u[:])
+    d_x1 = load("y", "ldx1", T.xin[:, 1024:2048], T.x[:, 1024:2048])
+    d_w = load("y", "ldw", T.wq[:].bitcast(dt.uint8), T.wc[:])
+    d_ws = load("y", "ldws", T.wsc[:], T.ws[:])
+    d_v = load("y", "ldv", T.vin[:], T.v[:])
+
+    t_pI = done("g", g.iota(T.pI[:], [[0, 1]], 0, 1))
+    t_ones = vec([], V.memset, T.ones[:], 1.0)
+    t_bu = vec([], V.memset, T.bu[:], 0.0)
+    t_g8 = iota(T.g8[:], [[1, 8]])
+    iota(T.gg[:], [[1, 4], [0, 2]])
+    t_gp = iota(T.gp[:], [[0, 4], [1, 2]])
+    t_m0 = select([t_ones], T.m0[:], T.ones[:, 0:128], [[0, 32], [1, 4]], OP.is_equal)
+    t_me = select([], T.me[:], T.ones[:, 0:64], [[0, 4], [1, 4], [-1, 4]], OP.is_equal)
+    t_iot = iota(T.iot[:], [[1, 32]])
+    t_w4 = iota(T.w4[:], [[0, 32], [1, 4]])
+    t_cs8 = iota(T.cs8[:], [[256, 16], [0, 2]], 6)
+    t_idc = iota(T.idc[:], [[8, 512]], 8)
+    for j in range(2):
+        t_rs = select([], T.rs[:, 512 * j:512 * j + 512], T.ones[:], [[0, 32], [1, 16]], OP.not_equal)
+
+    for j, (sh, am) in enumerate([(0, 15), (0, 31), (4, 7), (2, 3), (5, 3)]):
+        t_k = ts([t_pI], T.pK[:, j:j + 1], T.pI[:], sh, am, OP.logical_shift_right, OP.bitwise_and)
+    t_b = vec([], V.memset, T.tw[:, 3:4], -11.0 * LN2)
+    t_pF = vec([t_k], V.tensor_copy, T.pF[:], T.pK[:])
+    t_wb = act([t_pF, t_b], T.wx[:], T.pF[:, 0:1], AF.Exp, bias=T.tw[:, 3:4], scale=LN2)
+    t_gm = ts([t_pF, t_g8], T.gm[:], T.g8[:], T.pF[:, 2:3], None, OP.is_equal)
+    t1 = ts([], T.tw[:, 0:1], T.pF[:, 0:1], 10.0, None, OP.is_lt)
+    t2 = ts([], T.tw[:, 1:2], T.pF[:, 0:1], 10.0, None, OP.is_ge)
+    t3 = ts([], T.tw[:, 2:3], T.pF[:, 0:1], 12.0, None, OP.is_lt)
+    t_ba = ts([t_gp], T.ba[:], T.gg[:], T.pF[:, 4:5], None, OP.is_equal)
+    t_w8 = ts([t_wb, t1, t_gm], T.w8a[:], T.gm[:], T.wx[:, 0:1], T.tw[:, 0:1], OP.mult, OP.mult)
+    t4 = ts([t3], T.wxh[:], T.tw[:, 1:2], T.tw[:, 2:3], T.wx[:, 0:1], OP.mult, OP.mult)
+    t_ba1 = tt([t_ba], T.ba1[:], T.ba[:], T.gp[:], OP.mult)
+    t_w8h = ts([t4], T.w8h[:], T.gm[:], T.wxh[:, 0:1], 2.0, OP.mult, OP.mult)
+    t_w8n = ts([t4], T.w8n[:], T.gm[:], T.wxh[:, 0:1], -1.0, OP.mult, OP.mult)
+    t_ba0 = tt([t_ba1], T.ba0[:], T.ba[:], T.ba1[:], OP.subtract)
+    for a in range(4):
+        for par in range(2):
+            c = 512 * par + 128 * a
+            t_cA = act([t_w8, t_m0], T.cc[:, c:c + 128], T.m0[:], scale=T.w8a[:, 2 * a + par:2 * a + par + 1])
+    for k in range(8):
+        t_cW = ts([t_me, t_w8], T.cc[:, 1024 + 64 * k:1088 + 64 * k], T.me[:], T.w8a[:, k:k + 1], None, OP.mult)
+    for k in range(8):
+        act([t_w8n], T.cc[:, 2560 + 64 * k:2624 + 64 * k], T.m0[:, 0:64], scale=T.w8n[:, k:k + 1])
+    for k in range(8):
+        t_cR1 = act([t_ba1, t_me], T.cc[:, 2048 + 64 * k:2112 + 64 * k], T.me[:], scale=T.ba1[:, k:k + 1])
+    for k in range(8):
+        t_cH = act([t_w8h], T.cc[:, 3072 + 64 * k:3136 + 64 * k], T.me[:], scale=T.w8h[:, k:k + 1])
+
+    t_uq = vec([d_u], V.quantize_mx, T.uq[:], T.us[:], T.uin[:])
+    vec([d_x0], V.quantize_mx, T.xq_0[:, 0:256], T.xs_0[:, 0:256], T.xin[:, 0:1024])
+    t_qx = vec([d_x1], V.quantize_mx, T.xq_0[:, 256:512], T.xs_0[:, 256:512], T.xin[:, 1024:2048])
+
+    def more_constants():
+        for k in range(8):
+            tr = ts([t_ba0], T.cc[:, 1536 + 64 * k:1600 + 64 * k], T.me[:], T.ba0[:, k:k + 1], None, OP.mult)
+        late["kA"] = vec([t_cA, t_cW], V.quantize_mx, T.kq[:, 0:384], T.ks[:, 0:384], T.cc[:, 0:1536])
+        late["kR"] = vec([tr, t_cR1], V.quantize_mx, T.kq[:, 384:768], T.ks[:, 384:768], T.cc[:, 1536:3072])
+        t = ts([t_iot], T.mp[:, 0:32], T.iot[:], T.pF[:, 1:2], 4.0, OP.is_ge, OP.mult)
+        w = 32
+        while w < 512:
+            t = vec([t], V.tensor_copy, T.mp[:, w:2 * w], T.mp[:, 0:w])
+            w *= 2
+        late["mp"] = t
+        late["mk4"] = ts([t_w4], T.mk4[:], T.w4[:], T.pF[:, 3:4], None, OP.is_equal)
+        ts([], T.dc[:, 0:1], T.pF[:, 0:1], 2.0, 1024.0, OP.mult, OP.add)
+        late["dc"] = ts([], T.dc[:, 1:2], T.pF[:, 0:1], 2.0, 1025.0, OP.mult, OP.add)
+
+    def last_constants():
+        late["kH"] = vec([t_cH], V.quantize_mx, T.kq[:, 768:896], T.ks[:, 768:896], T.cc[:, 3072:3584])
+        late["mk0"] = ts([], T.mk[:, 0:16], T.iot[:, 0:16], T.pF[:, 0:1], None, OP.is_equal)
+        late["tab0"] = vec([], V.memset, T.tab_0[:, 0:1024], 2.5)
+
+    def masks(t):
+        w = 16
+        while w < 1024:
+            t = act([t], T.mk[:, w:2 * w], T.mk[:, 0:w])
+            w *= 2
+        late["mk"] = act([t], T.mk[:, 1024:1536], T.mk[:, 0:512], scale=512.0)
+
+    def unpackers():
+        for b in range(4):
+            late["ce"] = select([], T.ce[:, 512 * b:512 * b + 512], T.ones[:], [[-1, 512]], OP.is_equal, b, 4)
+
+    def later_constants():
+        late["ke"] = vec([late["ce"]], V.quantize_mx, T.eq[:], T.es[:], T.ce[:])
+        late["dz"] = vec([], V.memset, T.dw[:, 0:2112:528], 0.0)
+        late["tab1"] = vec([], V.memset, T.tab_1[:, 0:1024], 2.5)
+        late["vq"] = vec([d_v], V.quantize_mx, T.vq[:], T.vs[:], T.vin[:])
+
+    def k(i):
+        return T.kq[:, 128 * i:128 * i + 128], T.ks[:, 128 * i:128 * i + 128]
+
+    ein = {p: len(topo.engines(p, core)) for p in (prv, nxt)}
+    free = {"psS": None, "psM": None, "psA": None, "psR": None}
+
+    for t in range(ROUNDS):
+        B = lambda name, t=t: T["%s_%d" % (name, t)]
+        xq, xs, P, tab, la, hq = B("xq"), B("xs"), T.P, B("tab"), B("la"), B("hq")
+        r_b = [None] * 4
+
+        def layer(b):
+            r_b[b] = mm([d_w, d_ws, free["psR"]], T.psR[:, 512 * b:512 * b + 512], T.wq[:, 128 * b:128 * b + 128], T.wsc[:, 128 * b:128 * b + 128], xq[:], xs[:])
+
+        s_1 = mm([t_qx, t_uq, free["psS"]], T.psS[:], T.uq[:], T.us[:], xq[:], xs[:])
+        s_2 = mm([free["psM"]], T.psM[:], T.uq[:], T.us[:], xq[:], xs[:])
+        layer(0)
+        layer(1)
+        t_sg = act([s_1, t_bu], T.bu[:, 0:2048:4], T.psS[:], AF.Sign, bias=7.7e-34)
+        if t == 0:
+            more_constants()
+        t_bq = ts([s_2], T.bq[:], T.psM[:], 0.0, None, OP.is_lt)
+        q_bu = vec([t_sg], V.quantize_mx, T.buq[:], T.bus[:], T.bu[:])
+        q_bq = vec([t_bq], V.quantize_mx, T.bqq[:], T.bqs[:], T.bq[:])
+        if t == 0:
+            last_constants()
+        A0 = mm([q_bu, late["kA"], free["psA"]], T.psA[:, 0:512], *k(0), T.buq[:], T.bus[:])
+        A1 = mm([], T.psA[:, 512:1024], *k(1), T.buq[:], T.bus[:])
+        WA = mm([q_bq], T.psM[:, 0:128], *k(2), T.bqq[:], T.bqs[:])
+        H = mm([t_sg, late["kR"]], T.psS[:], *k(5), T.buq[:], T.bus[:])
+        layer(2)
+        layer(3)
+        t_P = [act([r_b[b]], P[:, b:2048:4], T.psR[:, 512 * b:512 * b + 512], scale=0.03125) for b in range(4)]
+        if t == 0:
+            masks(late["mk0"])
+        a0 = tt([A0, late["mp"]], T.AA[:], T.psA[:, 0:512], T.mp[:], OP.add)
+        a1 = tt([A1], T.AB[:], T.psA[:, 512:1024], T.mp[:], OP.add)
+        x0 = vec([a0], V.transpose, T.TA[:], T.AA[:])
+        w1 = tt([WA, late["mk4"]], T.e1[:], T.psM[:, 0:128], T.mk4[:], OP.mult)
+        x1 = vec([a1], V.transpose, T.TB[:], T.AB[:])
+        w2 = tt([w1], T.e2[:], T.e1[:, 0:128:2], T.e1[:, 1:128:2], OP.add)
+        WH = mm([w1, late["kH"]], T.psM[:, 0:128], *k(6), T.bqq[:], T.bqs[:])
+        e0 = tt([x0], T.EA[:], T.psA[:, 0:512], T.TA[:], OP.is_equal)
+        aw = tt([w2], T.aw[:], T.e2[:, 0:64:2], T.e2[:, 1:64:2], OP.add)
+        q0 = vec([e0], V.quantize_mx, T.eqa[:], T.esa[:], T.EA[:])
+        mm([e0], T.psA[:, 0:128], *k(2), T.bqq[:], T.bqs[:], True, False)
+        mm([q0], T.psA[:, 0:128], *k(3), T.eqa[:], T.esa[:], False, False)
+        e1 = tt([x1], T.EB[:], T.psA[:, 512:1024], T.TB[:], OP.is_equal)
+        i1 = ts([aw], T.i1[:], T.aw[:], 2048.0, 1.0, OP.mult, OP.add)
+        q1 = vec([e1], V.quantize_mx, T.eqb[:], T.esb[:], T.EB[:])
+        Y = mm([q1], T.psA[:, 0:128], *k(4), T.eqb[:], T.esb[:], False, True)
+        l0 = ts([aw], la[:, 0:32], T.aw[:], 2048.0, None, OP.mult)
+        i2 = ts([i1], T.i2[:], T.i1[:], 1023, None, OP.bitwise_and)
+        h1 = tt([WH], T.h1[:], T.psM[:, 0:128], T.mk4[:], OP.mult)
+        free["psM"] = h1
+        l1 = vec([i2], V.tensor_copy, la[:, 32:64], T.i2[:])
+        h2 = tt([h1], T.h2[:], T.h1[:, 0:128:2], T.h1[:, 1:128:2], OP.add)
+        y1 = tt([Y], T.y1[:], T.psA[:, 0:128], T.mk4[:], OP.mult)
+        free["psA"] = y1
+        hq0 = tt([h2], hq[:, 0:32], T.h2[:, 0:64:2], T.h2[:, 1:64:2], OP.add)
+        y2 = tt([y1], T.y2[:], T.y1[:, 0:128:2], T.y1[:, 1:128:2], OP.add)
+        hq1 = vec([hq0], V.tensor_copy, hq[:, 32:64], hq[:, 0:32])
+        yw = tt([y2], T.yw[:], T.y2[:, 0:64:2], T.y2[:, 1:64:2], OP.add)
+        vv = tt([H, t_idc], T.vv[:], T.psS[:], T.idc[:], OP.add)
+        free["psS"] = vv
+        for c in range(2):
+            o1 = ts([yw, late["dc"]], T.of1[:, c:32:2], T.yw[:, c:32:2], 2048.0, T.dc[:, c:c + 1], OP.mult, OP.min)
+        q_P = vec(t_P, V.quantize_mx, B("pq")[:], B("psc")[:], P[:])
+        need("g", [l0, l1, hq1])
+        rid, pid = topo.addr(nxt)[:2]
+        es = topo.engines(core, nxt)
+        half = len(es) // 2
+        g.remote_dma_fused([RemoteDMATransfer(dst_ids=[DstId(rid=rid, pnc=pid)], dma_engine_mask=bits(e), remote_sem=T.sem["gotq%d" % t], src=s, dst=d)
+                            for e, s, d in ((es[:half], la[:], B("ql")[:]), (es[half:], hq[:], B("qh")[:]))], local_sem=T.sem.sent)
+        sent[0] += len(es)
+        remote([q_P], prv, B("lc")[:].bitcast(dt.uint8), B("pq")[:].bitcast(dt.uint8), "gotc%d" % t)
+        remote([q_P], prv, B("ls")[:], B("psc")[:], "gotc%d" % t)
+        if t == 0:
+            unpackers()
+        sc = late["tab%d" % t]
+        for b in range(15, -1, -1):
+            sc = vec([sc, o1, vv], V.tensor_copy, tab[:, 0:1056].indirect(T.of1[:, 2 * b:2 * b + 2]), T.vv[:, 32 * b:32 * b + 32])
+        f1 = ts([i2], T.a1[:], T.i2[:], -1280.0, None, OP.add)
+        rk = tt([yw, aw], T.rk[:], T.yw[:], T.aw[:], OP.subtract)
+        fe = tt([sc, l1, l0, late["mk"]], T.FE[:], tab[:, 0:1024].indirect(la[:]), T.mk[:, 512:1536], OP.mult)
+        ss = vec([fe, t_rs], V.tensor_tensor_scan, T.SC[:], T.rs[:], T.FE[:], 0.0, OP.mult, OP.add)
+        g1 = tt([ss, t_cs8], T.s1[:], T.SC[:, 15:512:16], T.cs8[:], OP.is_ge)
+        u2 = tt([f1], T.s4[:], T.SC[:, 527:1024:16], T.a1[:], OP.add)
+        n1 = tt([g1, rk], T.s3[:], T.rk[:], T.s1[:], OP.not_equal)
+        n2 = ts([n1], T.s6[:], T.s3[:], 2048.0, None, OP.mult)
+        n3 = tt([n2, u2], T.s5[:], T.s6[:], T.s4[:], OP.add)
+        for c in range(2):
+            o2 = ts([n3], T.of2[:, c:32:2], T.s5[:, c:32:2], T.dc[:, c:c + 1], None, OP.min)
+        if t == 0:
+            later_constants()
+        sc = None
+        for b in range(15, -1, -1):
+            sc = vec([sc, o2, fe], V.tensor_copy, tab[:, 0:1056].indirect(T.of2[:, 2 * b:2 * b + 2]), T.vv[:, 32 * b:32 * b + 32])
+        got_q = ("gotq%d" % t, ein[prv])
+        ql, qh = B("ql"), B("qh")
+        ts([got_q], T.qf[:, 0:32], qh[:, 0:32], -8193.5, None, OP.add)
+        f_b = ts([], T.qf[:, 32:64], qh[:, 32:64], -1.5, None, OP.add)
+        sg = tt([sc, got_q], T.FG[:], tab[:, 0:1024].indirect(ql[:]), T.mk[:, 0:1024], OP.mult)
+        sd = vec([sg], V.tensor_tensor_scan, T.SD[:], T.rs[:], T.FG[:], 0.0, OP.mult, OP.add)
+        z1 = tt([sd, f_b], T.r1[:], T.SD[:, 15:1024:16], T.qf[:], OP.subtract)
+        z2 = ts([z1], T.r2[:], T.r1[:], 7, None, OP.bitwise_and)
+        z3 = ts([z2], T.r3[:], T.r2[:], 0.0, 0.125, OP.is_equal, OP.mult)
+        z4 = tt([z3], T.r4[:], T.r1[:], T.r3[:], OP.mult)
+        z5 = tt([z4], T.r5[:], T.r4[:, 0:32], T.r4[:, 32:64], OP.max)
+        z6 = ts([z5], T.r6[:], T.r5[:], 1023, None, OP.bitwise_and)
+        z7 = vec([z6], V.tensor_copy, B("lo")[:], T.r6[:])
+        remote([z7], prv, B("li")[:], B("lo")[:], "gotl%d" % t)
+        got_c = ("gotc%d" % t, 2 * ein[nxt])
+        for b in range(4):
+            D = mm([t_P[b], late["ke"], got_c], T.psR[:, 512 * b:512 * b + 512], T.eq[:, 128 * b:128 * b + 128], T.es[:, 128 * b:128 * b + 128], B("lc")[:], B("ls")[:])
+            free["psR"] = act([D, late["dz"]], T.dw[:, 528 * b + 1:528 * b + 513], T.psR[:, 512 * b:512 * b + 512])
+        X = T["X%d" % (t + 1)]
+        got_l = ("gotl%d" % t, ein[nxt])
+        for b in range(4):
+            xn = tt([got_l, free["psR"]], X[:, b:2048:4], T.dw[:, 528 * b:528 * b + 513].indirect(B("li")[:]), P[:, b:2048:4], OP.add)
+        xq, xs = T["xq_%d" % (t + 1)], T["xs_%d" % (t + 1)]
+        t_qx = vec([xn], V.quantize_mx, xq[:], xs[:], X[:])
+
+    need("y", [t_qx])
+    g.sync.dma_start(T.oc[:], xq[:].bitcast(dt.uint8)).then_inc(T.sem.stc, 16)
+    need("a", [t_qx])
+    for j in range(4):
+        S.dma_start(T.osc[4 * j:4 * j + 4, :], xs[32 * j:32 * j + 4, :]).then_inc(T.sem.sts, 16)
+    ym = mm([t_qx, late["vq"], free["psS"]], T.psS[:], T.vq[:], T.vs[:], xq[:], xs[:])
+    yo = vec([ym], V.tensor_copy, T.yo[:], T.psS[:])
+    need("y", [yo])
+    g.sync.dma_start(T.y[:], T.yo[:]).then_inc(T.sem.sty, 16)
+    need("g", [(s, c) for s, c in count.items()])
+    g.wait_ge(T.sem.sent, sent[0])
+    g.sync.wait_ge(T.sem.stc, 16)
+    g.sync.wait_ge(T.sem.sty, 16)
+    S.wait_ge(T.sem.sts, 64)

@@ -2,25 +2,26 @@ import numpy as np
 from concourse.bass import DstId, RemoteDMATransfer
 from concourse.mybir import dt, AluOpType as OP, ActivationFunctionType as AF
 
-F32, BF, I32, U16, U8, MX = "float32", "bfloat16", "int32", "uint16", "uint8", "float8_e4m3fn_x4"
+F32, F16, BF, I32, U16, U8, MX = "float32", "float16", "bfloat16", "int32", "uint16", "uint8", "float8_e4m3fn_x4"
 ROUNDS = 2
 LN2 = float(np.log(2.0))
 SCRATCH = {"psR": ("psum", [128, 2048], F32), "psS": ("psum", [128, 512], F32), "psM": ("psum", [128, 512], F32), "psA": ("psum", [128, 1024], F32)}
 for _d, _s in [
-    (BF, "xin 2048 X1 2048 X2 2048 uin 512 vin 512 P 2048 dw 2112 ones 512 me 64 m0 128 cc 3584 ce 2048 mk 1536 rs 1024 bu 2048 bq 512 EA 512 EB 512 hq_0 64 hq_1 64 qh_0 64 qh_1 64"),
-    (MX, "uq 128 vq 128 wq 512 kq 896 eq 512 xq_0 512 xq_1 512 xq_2 512 buq 512 bqq 128 eqa 128 eqb 128 pq_0 512 pq_1 512 lc_0 512 lc_1 512"),
-    (U8, "us 128 vs 128 wsc 512 ks 896 es 512 xs_0 512 xs_1 512 xs_2 512 bus 512 bqs 128 esa 128 esb 128 psc_0 512 psc_1 512 ls_0 512 ls_1 512"),
-    (F32, "yo 512 pF 5 iot 32 w4 128 g8 8 gg 8 gp 8 gm 8 wx 1 wxh 1 tw 4 w8a 8 w8h 8 w8n 8 ba 8 ba0 8 ba1 8 mk4 128 mp 512 idc 512 cs8 32 dc 2 "
-          "AA 512 AB 512 TA 512 TB 512 e1 128 e2 64 aw 32 a1 32 h1 128 h2 64 vv 512 y1 128 y2 64 yw 32 rk 32 tab_0 1056 tab_1 1056 "
-          "FE 1024 SC 1024 FG 1024 SD 1024 s1 32 s3 32 s4 32 s5 32 s6 32 qf 64 r3 64 r4 64"),
+    (BF, "xin 2048 X1 2048 X2 2048 uin 512 vin 512 P 2048 dw 2112 ones 512 me 64 m0 128 cc 4096 ce 2048 mk 512 rs 512 bu 2048 bq 512 EA 512 EB 512 GG 512 EE 512"),
+    (MX, "uq 128 vq 128 wq 512 kq 1024 eq 512 xq_0 512 xq_1 512 xq_2 512 buq 512 bqq 128 eqa 128 eqb 128 pq_0 512 pq_1 512 lc_0 512 lc_1 512 gq 128 nq 128"),
+    (U8, "us 128 vs 128 wsc 512 ks 1024 es 512 xs_0 512 xs_1 512 xs_2 512 bus 512 bqs 128 esa 128 esb 128 psc_0 512 psc_1 512 ls_0 512 ls_1 512 gsc 128 nsc 128"),
+    (F16, "AA 512 AB 512 TA 512 TB 512"),
+    (F32, "yo 512 pF 5 iot 512 w4 128 g8 8 gg 8 gp 8 gm 8 wx 1 wxh 1 tw 4 w8a 8 w8n 8 ba 8 ba0 8 ba1 8 mk4 128 mp 512 idc 512 cs8 512 dc 4 "
+          "e1 128 e2 64 aw 32 h1 128 h2 64 vv 512 y1 128 y2 64 yw 32 tab_0 1056 tab_1 1056 "
+          "FG 1024 SD 1024 g1 128 g2 64 gw 32 s5 32 s6 32 qf 64 r3 64 r4 64 hq_0 32 hq_1 32 qh_0 32 qh_1 32"),
     (I32, "pI 1 pK 5 i1 32 i2 32 r1 64 r2 64 r5 32 r6 32"),
     (U16, "la_0 64 la_1 64 of1 32 of2 32 ql_0 64 ql_1 64 lo_0 32 lo_1 32 li_0 32 li_1 32"),
 ]:
     _s = _s.split()
     for _i in range(0, len(_s), 2):
         SCRATCH[_s[_i]] = ("sbuf", [128, int(_s[_i + 1])], _d)
-SEMAPHORES = ["sv", "sa", "sp", "sg", "ldx0", "ldx1", "ldu", "ldv", "ldw", "ldws", "sty", "stc", "sts", "sent",
-              "gotq0", "gotq1", "gotc0", "gotc1", "gotl0", "gotl1"]
+SEMAPHORES = ["sv", "sa", "sp", "sg", "ldx0", "ldx1", "ldu", "ldv", "ldw", "ldws", "sty0", "sty1", "stc0", "stc1", "sts", "sent",
+              "gotq0", "gotq1", "gotc0", "gotc1", "gotl00", "gotl01", "gotl10", "gotl11"]
 
 
 def rank_program(g, core, T, topo):
@@ -74,7 +75,8 @@ def rank_program(g, core, T, topo):
         need("g", deps)
         return done("g", g.affine_select(out, in_, pattern, op, 0.0, base, cm))
 
-    def load(q, sem, out, in_):
+    def dma(q, sem, out, in_, deps=()):
+        need(q, deps)
         queue[q].dma_start(out, in_).then_inc(T.sem[sem], 16)
         return (sem, 16)
 
@@ -90,232 +92,282 @@ def rank_program(g, core, T, topo):
         g.remote_dma(out, in_, T.sem[sem], T.sem.sent, pid, rid, topo.mask(core, dst))
         sent[0] += len(topo.engines(core, dst))
 
-    d_x0 = load("y", "ldx0", T.xin[:, 0:1024], T.x[:, 0:1024])
-    d_u = load("a", "ldu", T.uin[:], T.u[:])
-    d_x1 = load("y", "ldx1", T.xin[:, 1024:2048], T.x[:, 1024:2048])
-    d_w = load("y", "ldw", T.wq[:].bitcast(dt.uint8), T.wc[:])
-    d_ws = load("y", "ldws", T.wsc[:], T.ws[:])
-    d_v = load("y", "ldv", T.vin[:], T.v[:])
+    d_x = [dma("y", "ldx0", T.xin[:, 0:1024], T.x[:, 0:1024])]
+    d_u = dma("a", "ldu", T.uin[:], T.u[:])
+    d_x.append(dma("y", "ldx1", T.xin[:, 1024:2048], T.x[:, 1024:2048]))
+    d_w = dma("y", "ldw", T.wq[:].bitcast(dt.uint8), T.wc[:])
+    d_ws = dma("y", "ldws", T.wsc[:], T.ws[:])
+    d_v = dma("y", "ldv", T.vin[:], T.v[:])
 
     t_pI = done("g", g.iota(T.pI[:], [[0, 1]], 0, 1))
     t_ones = vec([], V.memset, T.ones[:], 1.0)
-    t_bu = vec([], V.memset, T.bu[:], 0.0)
     t_g8 = iota(T.g8[:], [[1, 8]])
     iota(T.gg[:], [[1, 4], [0, 2]])
     t_gp = iota(T.gp[:], [[0, 4], [1, 2]])
     t_m0 = select([t_ones], T.m0[:], T.ones[:, 0:128], [[0, 32], [1, 4]], OP.is_equal)
     t_me = select([], T.me[:], T.ones[:, 0:64], [[0, 4], [1, 4], [-1, 4]], OP.is_equal)
-    t_iot = iota(T.iot[:], [[1, 32]])
     t_w4 = iota(T.w4[:], [[0, 32], [1, 4]])
-    t_cs8 = iota(T.cs8[:], [[256, 16], [0, 2]], 6)
-    t_idc = iota(T.idc[:], [[8, 512]], 8)
-    for j in range(2):
-        t_rs = select([], T.rs[:, 512 * j:512 * j + 512], T.ones[:], [[0, 32], [1, 16]], OP.not_equal)
-
-    for j, (sh, am) in enumerate([(0, 15), (0, 31), (4, 7), (2, 3), (5, 3)]):
-        t_k = ts([t_pI], T.pK[:, j:j + 1], T.pI[:], sh, am, OP.logical_shift_right, OP.bitwise_and)
-    t_b = vec([], V.memset, T.tw[:, 3:4], -11.0 * LN2)
-    t_pF = vec([t_k], V.tensor_copy, T.pF[:], T.pK[:])
-    t_wb = act([t_pF, t_b], T.wx[:], T.pF[:, 0:1], AF.Exp, bias=T.tw[:, 3:4], scale=LN2)
-    t_gm = ts([t_pF, t_g8], T.gm[:], T.g8[:], T.pF[:, 2:3], None, OP.is_equal)
-    t1 = ts([], T.tw[:, 0:1], T.pF[:, 0:1], 10.0, None, OP.is_lt)
-    t2 = ts([], T.tw[:, 1:2], T.pF[:, 0:1], 10.0, None, OP.is_ge)
-    t3 = ts([], T.tw[:, 2:3], T.pF[:, 0:1], 12.0, None, OP.is_lt)
-    t_ba = ts([t_gp], T.ba[:], T.gg[:], T.pF[:, 4:5], None, OP.is_equal)
-    t_w8 = ts([t_wb, t1, t_gm], T.w8a[:], T.gm[:], T.wx[:, 0:1], T.tw[:, 0:1], OP.mult, OP.mult)
-    t4 = ts([t3], T.wxh[:], T.tw[:, 1:2], T.tw[:, 2:3], T.wx[:, 0:1], OP.mult, OP.mult)
-    t_ba1 = tt([t_ba], T.ba1[:], T.ba[:], T.gp[:], OP.mult)
-    t_w8h = ts([t4], T.w8h[:], T.gm[:], T.wxh[:, 0:1], 2.0, OP.mult, OP.mult)
-    t_w8n = ts([t4], T.w8n[:], T.gm[:], T.wxh[:, 0:1], -1.0, OP.mult, OP.mult)
-    t_ba0 = tt([t_ba1], T.ba0[:], T.ba[:], T.ba1[:], OP.subtract)
-    for a in range(4):
-        for par in range(2):
-            c = 512 * par + 128 * a
-            t_cA = act([t_w8, t_m0], T.cc[:, c:c + 128], T.m0[:], scale=T.w8a[:, 2 * a + par:2 * a + par + 1])
-    for k in range(8):
-        t_cW = ts([t_me, t_w8], T.cc[:, 1024 + 64 * k:1088 + 64 * k], T.me[:], T.w8a[:, k:k + 1], None, OP.mult)
-    for k in range(8):
-        act([t_w8n], T.cc[:, 2560 + 64 * k:2624 + 64 * k], T.m0[:, 0:64], scale=T.w8n[:, k:k + 1])
-    for k in range(8):
-        t_cR1 = act([t_ba1, t_me], T.cc[:, 2048 + 64 * k:2112 + 64 * k], T.me[:], scale=T.ba1[:, k:k + 1])
-    for k in range(8):
-        t_cH = act([t_w8h], T.cc[:, 3072 + 64 * k:3136 + 64 * k], T.me[:], scale=T.w8h[:, k:k + 1])
-
-    t_uq = vec([d_u], V.quantize_mx, T.uq[:], T.us[:], T.uin[:])
-    vec([d_x0], V.quantize_mx, T.xq_0[:, 0:256], T.xs_0[:, 0:256], T.xin[:, 0:1024])
-    t_qx = vec([d_x1], V.quantize_mx, T.xq_0[:, 256:512], T.xs_0[:, 256:512], T.xin[:, 1024:2048])
-
-    def more_constants():
-        for k in range(8):
-            tr = ts([t_ba0], T.cc[:, 1536 + 64 * k:1600 + 64 * k], T.me[:], T.ba0[:, k:k + 1], None, OP.mult)
-        late["kA"] = vec([t_cA, t_cW], V.quantize_mx, T.kq[:, 0:384], T.ks[:, 0:384], T.cc[:, 0:1536])
-        late["kR"] = vec([tr, t_cR1], V.quantize_mx, T.kq[:, 384:768], T.ks[:, 384:768], T.cc[:, 1536:3072])
-        t = ts([t_iot], T.mp[:, 0:32], T.iot[:], T.pF[:, 1:2], 4.0, OP.is_ge, OP.mult)
-        w = 32
-        while w < 512:
-            t = vec([t], V.tensor_copy, T.mp[:, w:2 * w], T.mp[:, 0:w])
-            w *= 2
-        late["mp"] = t
-        late["mk4"] = ts([t_w4], T.mk4[:], T.w4[:], T.pF[:, 3:4], None, OP.is_equal)
-        ts([], T.dc[:, 0:1], T.pF[:, 0:1], 2.0, 1024.0, OP.mult, OP.add)
-        late["dc"] = ts([], T.dc[:, 1:2], T.pF[:, 0:1], 2.0, 1025.0, OP.mult, OP.add)
-
-    def last_constants():
-        late["kH"] = vec([t_cH], V.quantize_mx, T.kq[:, 768:896], T.ks[:, 768:896], T.cc[:, 3072:3584])
-        late["mk0"] = ts([], T.mk[:, 0:16], T.iot[:, 0:16], T.pF[:, 0:1], None, OP.is_equal)
-        late["tab0"] = vec([], V.memset, T.tab_0[:, 0:1024], 2.5)
-
-    def masks(t):
-        w = 16
-        while w < 1024:
-            t = act([t], T.mk[:, w:2 * w], T.mk[:, 0:w])
-            w *= 2
-        late["mk"] = act([t], T.mk[:, 1024:1536], T.mk[:, 0:512], scale=512.0)
+    t_iot = iota(T.iot[:], [[0, 16], [1, 32]])
+    tabs = [iota(T.tab_0[:, 0:1024], [[0, 1024]], 5)]
+    t_idc = iota(T.idc[:], [[16, 512]], 16)
+    t_cs8 = iota(T.cs8[:], [[512, 16], [0, 32]], 12)
+    t_rs = select([], T.rs[:], T.ones[:], [[0, 32], [1, 16]], OP.not_equal)
 
     def unpackers():
         for b in range(4):
             late["ce"] = select([], T.ce[:, 512 * b:512 * b + 512], T.ones[:], [[-1, 512]], OP.is_equal, b, 4)
 
-    def later_constants():
-        late["ke"] = vec([late["ce"]], V.quantize_mx, T.eq[:], T.es[:], T.ce[:])
-        late["dz"] = vec([], V.memset, T.dw[:, 0:2112:528], 0.0)
-        late["tab1"] = vec([], V.memset, T.tab_1[:, 0:1024], 2.5)
-        late["vq"] = vec([d_v], V.quantize_mx, T.vq[:], T.vs[:], T.vin[:])
+    t_b = vec([], V.memset, T.tw[:, 3:4], -LN2)
+    for j, (sh, am) in enumerate([(0, 15), (0, 31), (4, 7), (2, 3), (5, 3)]):
+        t_k = ts([t_pI], T.pK[:, j:j + 1], T.pI[:], sh, am, OP.logical_shift_right, OP.bitwise_and)
+    t_pF = vec([t_k], V.tensor_copy, T.pF[:], T.pK[:])
+    t_wb = act([t_pF, t_b], T.wx[:], T.pF[:, 0:1], AF.Exp, bias=T.tw[:, 3:4], scale=LN2)
+    t_gm = ts([t_pF, t_g8], T.gm[:], T.g8[:], T.pF[:, 2:3], None, OP.is_equal)
+    t1 = ts([], T.tw[:, 0:1], T.pF[:, 0:1], 10.0, -1.0, OP.is_lt, OP.mult)
+    t2 = ts([], T.tw[:, 1:2], T.pF[:, 0:1], 10.0, None, OP.is_ge)
+    t3 = ts([], T.tw[:, 2:3], T.pF[:, 0:1], 12.0, None, OP.is_lt)
+    t_ba = ts([t_gp], T.ba[:], T.gg[:], T.pF[:, 4:5], 2048.0, OP.is_equal, OP.mult)
+    t_bu = vec([], V.memset, T.bu[:], 0.0)
+    t_ba1 = tt([t_ba], T.ba1[:], T.ba[:], T.gp[:], OP.mult)
+    t_ba0 = tt([t_ba1], T.ba0[:], T.ba[:], T.ba1[:], OP.subtract)
+    t_w8 = ts([t_wb, t1, t_gm], T.w8a[:], T.gm[:], T.wx[:, 0:1], T.tw[:, 0:1], OP.mult, OP.mult)
+    t4 = ts([t3], T.wxh[:], T.tw[:, 1:2], T.tw[:, 2:3], T.wx[:, 0:1], OP.mult, OP.mult)
+    t_w8n = ts([t4], T.w8n[:], T.gm[:], T.wxh[:, 0:1], -1.0 / 512.0, OP.mult, OP.mult)
+    t_gm2 = ts([t_ba0], T.ba[:], T.gm[:], -128.0, None, OP.mult)
+    for a in range(4):
+        for par in range(2):
+            c = 512 * par + 128 * a
+            t_cA = ts([t_w8, t_m0], T.cc[:, c:c + 128], T.m0[:], T.w8a[:, 2 * a + par:2 * a + par + 1], None, OP.mult)
+
+    def fill(first, src, col, deps):
+        for q in range(8):
+            t_f = act(deps, T.cc[:, first + 64 * q:first + 64 * q + 64], src[:, 0:64], scale=col[:, q:q + 1])
+        return t_f
+
+    t_cW = fill(1024, T.me, T.w8a, [t_w8, t_me])
+    t_cF = fill(1536, T.m0, T.w8n, [t_w8n, t_m0])
+    for first, src in ((2048, T.ba0), (2560, T.ba1)):
+        for q in range(8):
+            t_cR = ts([t_ba0, t_me], T.cc[:, first + 64 * q:first + 64 * q + 64], T.me[:], src[:, q:q + 1], None, OP.mult)
+    vec([d_u], V.quantize_mx, T.uq[:], T.us[:], T.uin[:])
+    t_qx = [vec([d_x[h]], V.quantize_mx, T.xq_0[:, 256 * h:256 * h + 256], T.xs_0[:, 256 * h:256 * h + 256], T.xin[:, 1024 * h:1024 * h + 1024]) for h in range(2)]
+
+    def constants_1():
+        late["kA"] = vec([t_cA, t_cW], V.quantize_mx, T.kq[:, 0:384], T.ks[:, 0:384], T.cc[:, 0:1536])
+        late["mk4"] = ts([t_w4], T.mk4[:], T.w4[:], T.pF[:, 3:4], None, OP.is_equal)
+        late["mk0"] = ts([t_iot], T.mk[:, 0:16], T.iot[:, 0:16], T.pF[:, 0:1], None, OP.is_equal)
+
+    def constants_3():
+        fill(3072, T.me, T.w8n, [])
+        late["cG"] = fill(3584, T.me, T.ba, [t_gm2])
+        for j, base in enumerate((512.5, 513.5, 1024.0, 1025.0)):
+            late["dc"] = act([], T.dc[:, j:j + 1], T.pF[:, 0:1], AF.Copy, scale=2.0, bias=base)
+
+    def masks(t):
+        w = 16
+        while w < 512:
+            t = act([t], T.mk[:, w:2 * w], T.mk[:, 0:w])
+            w *= 2
+        late["mk"] = t
 
     def k(i):
         return T.kq[:, 128 * i:128 * i + 128], T.ks[:, 128 * i:128 * i + 128]
 
+    def lower(x):
+        return x[:, 0::2], x[:, 1::2]
+
     ein = {p: len(topo.engines(p, core)) for p in (prv, nxt)}
     free = {"psS": None, "psM": None, "psA": None, "psR": None}
+    half_bank = (T.psS, T.psM)
+    half = (slice(0, 256), slice(256, 512))
+    st = {}
+
+    def signs(t, h, dep):
+        xq, xs = T["xq_%d" % t], T["xs_%d" % t]
+        s = mm([dep, free["psS"], free["psM"]], half_bank[h][:, 0:256], T.uq[:], T.us[:], xq[:, half[h]], xs[:, half[h]])
+        st["sg", h] = act([s, t_bu], T.bu[:, 1024 * h:1024 * h + 1024:4], half_bank[h][:, 0:256], AF.Sign, bias=7.7e-34)
+        st["bq"] = act([], T.bq[:, half[h]], half_bank[h][:, 0:256], AF.Sign, bias=7.7e-34)
+
+    def bank(par, h):
+        return (T.psA, T.psR)[h][:, 512 * par:512 * par + 256]
+
+    def addresses(h):
+        q = vec([st["sg", h]], V.quantize_mx, T.buq[:, half[h]], T.bus[:, half[h]], T.bu[:, 1024 * h:1024 * h + 1024])
+        for par in range(2):
+            st["A", par, h] = mm([q, late["kA"], free["psA"], free["psR"]], bank(par, h), *k(par), T.buq[:, half[h]], T.bus[:, half[h]])
 
     for t in range(ROUNDS):
         B = lambda name, t=t: T["%s_%d" % (name, t)]
         xq, xs, P, tab, la, hq = B("xq"), B("xs"), T.P, B("tab"), B("la"), B("hq")
         r_b = [None] * 4
 
-        def layer(b):
-            r_b[b] = mm([d_w, d_ws, free["psR"]], T.psR[:, 512 * b:512 * b + 512], T.wq[:, 128 * b:128 * b + 128], T.wsc[:, 128 * b:128 * b + 128], xq[:], xs[:])
+        def layer(b, dep=None):
+            r_b[b] = mm([d_w, d_ws, free["psR"], dep], T.psR[:, 512 * b:512 * b + 512], T.wq[:, 128 * b:128 * b + 128], T.wsc[:, 128 * b:128 * b + 128], xq[:], xs[:])
 
-        s_1 = mm([t_qx, t_uq, free["psS"]], T.psS[:], T.uq[:], T.us[:], xq[:], xs[:])
-        s_2 = mm([free["psM"]], T.psM[:], T.uq[:], T.us[:], xq[:], xs[:])
-        layer(0)
-        layer(1)
-        t_sg = act([s_1, t_bu], T.bu[:, 0:2048:4], T.psS[:], AF.Sign, bias=7.7e-34)
+        def masked(par, h):
+            return tt([st["A", par, h], late["mp"]], (T.AA, T.AB)[par][:, half[h]], bank(par, h), T.mp[:, half[h]], OP.add)
+
+        def turned(par, h, dep):
+            return vec([dep], V.transpose, (T.TA, T.TB)[par][:, half[h]], (T.AA, T.AB)[par][:, half[h]])
+
+        def equal(par, h, dep):
+            return tt([dep], (T.EA, T.EB)[par][:, half[h]], bank(par, h), (T.TA, T.TB)[par][:, half[h]], OP.is_equal)
+
         if t == 0:
-            more_constants()
-        t_bq = ts([s_2], T.bq[:], T.psM[:], 0.0, None, OP.is_lt)
-        q_bu = vec([t_sg], V.quantize_mx, T.buq[:], T.bus[:], T.bu[:])
-        q_bq = vec([t_bq], V.quantize_mx, T.bqq[:], T.bqs[:], T.bq[:])
-        if t == 0:
-            last_constants()
-        A0 = mm([q_bu, late["kA"], free["psA"]], T.psA[:, 0:512], *k(0), T.buq[:], T.bus[:])
-        A1 = mm([], T.psA[:, 512:1024], *k(1), T.buq[:], T.bus[:])
-        WA = mm([q_bq], T.psM[:, 0:128], *k(2), T.bqq[:], T.bqs[:])
-        H = mm([t_sg, late["kR"]], T.psS[:], *k(5), T.buq[:], T.bus[:])
+            signs(0, 0, t_qx[0])
+            signs(0, 1, t_qx[1])
+            constants_3()
+            constants_1()
+            addresses(0)
+            late["mp"] = ts([t_iot], T.mp[:], T.iot[:], T.pF[:, 1:2], 4096.0, OP.is_ge, OP.mult)
         layer(2)
-        layer(3)
-        t_P = [act([r_b[b]], P[:, b:2048:4], T.psR[:, 512 * b:512 * b + 512], scale=0.03125) for b in range(4)]
+        a0, a1 = masked(0, 0), masked(1, 0)
+        x0, x1 = turned(0, 0, a0), turned(1, 0, a1)
+        addresses(1)
+        e00 = equal(0, 0, x0)
+        q_bq = vec([st["bq"]], V.quantize_mx, T.bqq[:], T.bqs[:], T.bq[:])
         if t == 0:
-            masks(late["mk0"])
-        a0 = tt([A0, late["mp"]], T.AA[:], T.psA[:, 0:512], T.mp[:], OP.add)
-        a1 = tt([A1], T.AB[:], T.psA[:, 512:1024], T.mp[:], OP.add)
-        x0 = vec([a0], V.transpose, T.TA[:], T.AA[:])
+            late["kR"] = vec([t_cF, t_cR], V.quantize_mx, T.kq[:, 384:768], T.ks[:, 384:768], T.cc[:, 1536:3072])
+        WA = mm([q_bq], T.psM[:, 0:128], *k(2), T.bqq[:], T.bqs[:])
+        layer(3)
+        H = mm([late["kR"]], T.psS[:], *k(3), T.buq[:], T.bus[:])
+        e10 = equal(1, 0, x1)
+        mm([e00], T.psA[:, 0:128], *k(2), T.bqq[:], T.bqs[:], True, False)
+        a0, a1 = masked(0, 1), masked(1, 1)
+        x0 = turned(0, 1, a0)
         w1 = tt([WA, late["mk4"]], T.e1[:], T.psM[:, 0:128], T.mk4[:], OP.mult)
-        x1 = vec([a1], V.transpose, T.TB[:], T.AB[:])
-        w2 = tt([w1], T.e2[:], T.e1[:, 0:128:2], T.e1[:, 1:128:2], OP.add)
-        WH = mm([w1, late["kH"]], T.psM[:, 0:128], *k(6), T.bqq[:], T.bqs[:])
-        e0 = tt([x0], T.EA[:], T.psA[:, 0:512], T.TA[:], OP.is_equal)
-        aw = tt([w2], T.aw[:], T.e2[:, 0:64:2], T.e2[:, 1:64:2], OP.add)
-        q0 = vec([e0], V.quantize_mx, T.eqa[:], T.esa[:], T.EA[:])
-        mm([e0], T.psA[:, 0:128], *k(2), T.bqq[:], T.bqs[:], True, False)
-        mm([q0], T.psA[:, 0:128], *k(3), T.eqa[:], T.esa[:], False, False)
-        e1 = tt([x1], T.EB[:], T.psA[:, 512:1024], T.TB[:], OP.is_equal)
-        i1 = ts([aw], T.i1[:], T.aw[:], 2048.0, 1.0, OP.mult, OP.add)
-        q1 = vec([e1], V.quantize_mx, T.eqb[:], T.esb[:], T.EB[:])
-        Y = mm([q1], T.psA[:, 0:128], *k(4), T.eqb[:], T.esb[:], False, True)
-        l0 = ts([aw], la[:, 0:32], T.aw[:], 2048.0, None, OP.mult)
-        i2 = ts([i1], T.i2[:], T.i1[:], 1023, None, OP.bitwise_and)
-        h1 = tt([WH], T.h1[:], T.psM[:, 0:128], T.mk4[:], OP.mult)
-        free["psM"] = h1
-        l1 = vec([i2], V.tensor_copy, la[:, 32:64], T.i2[:])
-        h2 = tt([h1], T.h2[:], T.h1[:, 0:128:2], T.h1[:, 1:128:2], OP.add)
-        y1 = tt([Y], T.y1[:], T.psA[:, 0:128], T.mk4[:], OP.mult)
-        free["psA"] = y1
-        hq0 = tt([h2], hq[:, 0:32], T.h2[:, 0:64:2], T.h2[:, 1:64:2], OP.add)
-        y2 = tt([y1], T.y2[:], T.y1[:, 0:128:2], T.y1[:, 1:128:2], OP.add)
-        hq1 = vec([hq0], V.tensor_copy, hq[:, 32:64], hq[:, 0:32])
-        yw = tt([y2], T.yw[:], T.y2[:, 0:64:2], T.y2[:, 1:64:2], OP.add)
+        e01 = equal(0, 1, x0)
+        x1 = turned(1, 1, a1)
+        q0 = vec([e01], V.quantize_mx, T.eqa[:], T.esa[:], T.EA[:])
+        mm([q0], T.psA[:, 0:128], *k(4), T.eqa[:], T.esa[:], False, False)
+        e11 = equal(1, 1, x1)
+        w2 = tt([w1], T.e2[:], *lower(T.e1), OP.add)
+        q1 = vec([e11], V.quantize_mx, T.eqb[:], T.esb[:], T.EB[:])
+        Y = mm([q1], T.psA[:, 0:128], *k(5), T.eqb[:], T.esb[:], False, True)
+        aw = tt([w2], T.aw[:], *lower(T.e2), OP.add)
         vv = tt([H, t_idc], T.vv[:], T.psS[:], T.idc[:], OP.add)
         free["psS"] = vv
+        if t == 0:
+            late["kG"] = vec([late["cG"]], V.quantize_mx, T.kq[:, 768:1024], T.ks[:, 768:1024], T.cc[:, 3072:4096])
+        WH = mm([w1, late["kG"]], T.psM[:, 0:128], *k(6), T.bqq[:], T.bqs[:])
+        layer(0, e01)
+        layer(1, e11)
+        t_P = [None] * 4
+        for b in (2, 3, 0, 1):
+            t_P[b] = act([r_b[b]], P[:, b:2048:4], T.psR[:, 512 * b:512 * b + 512], scale=0.03125)
+        if t == 0:
+            masks(late["mk0"])
+        y1 = tt([Y], T.y1[:], T.psA[:, 0:128], T.mk4[:], OP.mult)
+        i1 = ts([aw], T.i1[:], T.aw[:], 512.5, None, OP.add)
+        y2 = tt([y1], T.y2[:], *lower(T.y1), OP.add)
+        i2 = ts([i1], T.i2[:], T.i1[:], 1023, None, OP.bitwise_and)
+        yw = tt([y2], T.yw[:], *lower(T.y2), OP.add)
+        l0 = ts([aw], la[:, 0:16], T.aw[:, 0:16], 511.5, None, OP.add)
         for c in range(2):
-            o1 = ts([yw, late["dc"]], T.of1[:, c:32:2], T.yw[:, c:32:2], 2048.0, T.dc[:, c:c + 1], OP.mult, OP.min)
-        q_P = vec(t_P, V.quantize_mx, B("pq")[:], B("psc")[:], P[:])
-        need("g", [l0, l1, hq1])
+            o1 = ts([yw, late["dc"]], T.of1[:, c:32:2], T.yw[:, c:32:2], T.dc[:, c:c + 1], 511.5, OP.min, OP.add)
+        sc, hx = None, None
+        for j in range(16):
+            b = 15 - j
+            sc = vec([tabs[t], o1, vv, sc], V.tensor_copy, tab[:, 0:1056].indirect(T.of1[:, 2 * b:2 * b + 2]), T.vv[:, 32 * b:32 * b + 32])
+            if j < 2:
+                l1 = vec([i2], V.tensor_copy, la[:, 32 * j + 16:32 * j + 32], T.i2[:, 16 * j:16 * j + 16])
+            elif j == 2:
+                l0 = ts([aw], la[:, 32:48], T.aw[:, 16:32], 511.5, None, OP.add)
+            elif j == 3:
+                hx = free["psM"] = tt([WH], T.h1[:], T.psM[:, 0:128], T.mk4[:], OP.mult)
+            elif j == 4:
+                hx = tt([hx], T.h2[:], *lower(T.h1), OP.add)
+            elif j == 5:
+                hx = tt([hx], hq[:], *lower(T.h2), OP.add)
+            elif j == 9:
+                q_P = vec(t_P, V.quantize_mx, B("pq")[:], B("psc")[:], P[:])
+        need("g", [l0, l1, hx])
         rid, pid = topo.addr(nxt)[:2]
         es = topo.engines(core, nxt)
-        half = len(es) // 2
+        m = len(es) // 2
         g.remote_dma_fused([RemoteDMATransfer(dst_ids=[DstId(rid=rid, pnc=pid)], dma_engine_mask=bits(e), remote_sem=T.sem["gotq%d" % t], src=s, dst=d)
-                            for e, s, d in ((es[:half], la[:], B("ql")[:]), (es[half:], hq[:], B("qh")[:]))], local_sem=T.sem.sent)
+                            for e, s, d in ((es[:m], la[:], B("ql")[:]), (es[m:], hq[:], B("qh")[:]))], local_sem=T.sem.sent)
         sent[0] += len(es)
         remote([q_P], prv, B("lc")[:].bitcast(dt.uint8), B("pq")[:].bitcast(dt.uint8), "gotc%d" % t)
         remote([q_P], prv, B("ls")[:], B("psc")[:], "gotc%d" % t)
         if t == 0:
             unpackers()
-        sc = late["tab%d" % t]
-        for b in range(15, -1, -1):
-            sc = vec([sc, o1, vv], V.tensor_copy, tab[:, 0:1056].indirect(T.of1[:, 2 * b:2 * b + 2]), T.vv[:, 32 * b:32 * b + 32])
-        f1 = ts([i2], T.a1[:], T.i2[:], -1280.0, None, OP.add)
-        rk = tt([yw, aw], T.rk[:], T.yw[:], T.aw[:], OP.subtract)
-        fe = tt([sc, l1, l0, late["mk"]], T.FE[:], tab[:, 0:1024].indirect(la[:]), T.mk[:, 512:1536], OP.mult)
-        ss = vec([fe, t_rs], V.tensor_tensor_scan, T.SC[:], T.rs[:], T.FE[:], 0.0, OP.mult, OP.add)
-        g1 = tt([ss, t_cs8], T.s1[:], T.SC[:, 15:512:16], T.cs8[:], OP.is_ge)
-        u2 = tt([f1], T.s4[:], T.SC[:, 527:1024:16], T.a1[:], OP.add)
-        n1 = tt([g1, rk], T.s3[:], T.rk[:], T.s1[:], OP.not_equal)
-        n2 = ts([n1], T.s6[:], T.s3[:], 2048.0, None, OP.mult)
-        n3 = tt([n2, u2], T.s5[:], T.s6[:], T.s4[:], OP.add)
+            tabs.append(iota(T.tab_1[:, 0:1024], [[0, 1024]], 5))
+        for h in range(2):
+            em = act([sc, l1], T.EE[:, half[h]], tab[:, 0:1024].indirect(la[:, 32 * h + 16:32 * h + 32]), AF.Sign, bias=5.5, scale=-1.0)
+        for h in range(2):
+            fe = tt([sc, l0, t_cs8], T.GG[:, half[h]], tab[:, 0:1024].indirect(la[:, 32 * h:32 * h + 16]), T.cs8[:, half[h]], OP.is_ge)
+        q_g = vec([fe], V.quantize_mx, T.gq[:], T.gsc[:], T.GG[:])
+        q_e = vec([em], V.quantize_mx, T.nq[:], T.nsc[:], T.EE[:])
+        mm([e11], T.psA[:, 512:640], *k(4), T.eqa[:], T.esa[:], True, False)
+        mm([], T.psA[:, 512:640], *k(5), T.eqb[:], T.esb[:], False, False)
+        mm([q_g], T.psA[:, 512:640], *k(7), T.gq[:], T.gsc[:], False, False)
+        Z = mm([q_e], T.psA[:, 512:640], *k(7), T.nq[:], T.nsc[:], False, True)
+        n1 = tt([Z], T.g1[:], T.psA[:, 512:640], T.mk4[:], OP.mult)
+        free["psA"] = n1
+        n2 = tt([n1], T.g2[:], *lower(T.g1), OP.add)
+        n3 = tt([n2], T.gw[:], *lower(T.g2), OP.add)
+        n4 = ts([n3], T.s6[:], T.gw[:], -2048.0, 2048.0, OP.not_equal, OP.mult)
+        n5 = tt([n4], T.s5[:], T.s6[:], T.i2[:], OP.add)
         for c in range(2):
-            o2 = ts([n3], T.of2[:, c:32:2], T.s5[:, c:32:2], T.dc[:, c:c + 1], None, OP.min)
-        if t == 0:
-            later_constants()
-        sc = None
-        for b in range(15, -1, -1):
-            sc = vec([sc, o2, fe], V.tensor_copy, tab[:, 0:1056].indirect(T.of2[:, 2 * b:2 * b + 2]), T.vv[:, 32 * b:32 * b + 32])
+            o2 = ts([n5], T.of2[:, c:32:2], T.s5[:, c:32:2], T.dc[:, 2 + c:3 + c], None, OP.min)
         got_q = ("gotq%d" % t, ein[prv])
         ql, qh = B("ql"), B("qh")
-        ts([got_q], T.qf[:, 0:32], qh[:, 0:32], -8193.5, None, OP.add)
-        f_b = ts([], T.qf[:, 32:64], qh[:, 32:64], -1.5, None, OP.add)
-        sg = tt([sc, got_q], T.FG[:], tab[:, 0:1024].indirect(ql[:]), T.mk[:, 0:1024], OP.mult)
-        sd = vec([sg], V.tensor_tensor_scan, T.SD[:], T.rs[:], T.FG[:], 0.0, OP.mult, OP.add)
-        z1 = tt([sd, f_b], T.r1[:], T.SD[:, 15:1024:16], T.qf[:], OP.subtract)
-        z2 = ts([z1], T.r2[:], T.r1[:], 7, None, OP.bitwise_and)
-        z3 = ts([z2], T.r3[:], T.r2[:], 0.0, 0.125, OP.is_equal, OP.mult)
-        z4 = tt([z3], T.r4[:], T.r1[:], T.r3[:], OP.mult)
-        z5 = tt([z4], T.r5[:], T.r4[:, 0:32], T.r4[:, 32:64], OP.max)
-        z6 = ts([z5], T.r6[:], T.r5[:], 1023, None, OP.bitwise_and)
-        z7 = vec([z6], V.tensor_copy, B("lo")[:], T.r6[:])
-        remote([z7], prv, B("li")[:], B("lo")[:], "gotl%d" % t)
+        sc = None
+        for j in range(16):
+            b, h = 15 - j, j % 2
+            sc = vec([o2, em, sc], V.tensor_copy, tab[:, 0:1056].indirect(T.of2[:, 2 * b:2 * b + 2]), T.vv[:, 32 * b:32 * b + 32])
+            if t == 0 and j == 9:
+                late["dz"] = vec([], V.memset, T.dw[:, 0:2112:528], 0.0)
+            elif 10 <= j < 12:
+                ts([got_q], T.qf[:, 32 * h:32 * h + 16], qh[:, 16 * h:16 * h + 16], -16384.0, None, OP.add)
+            elif 12 <= j < 14:
+                f_b = vec([], V.tensor_copy, T.qf[:, 32 * h + 16:32 * h + 32], qh[:, 16 * h:16 * h + 16])
+            elif t == 0 and j == 14:
+                late["ke"] = vec([late["ce"]], V.quantize_mx, T.eq[:], T.es[:], T.ce[:])
+        for h in range(2):
+            w, c, o = slice(512 * h, 512 * h + 512), slice(32 * h, 32 * h + 32), slice(16 * h, 16 * h + 16)
+            sg = tt([sc, got_q, late["mk"]], T.FG[:, w], tab[:, 0:1024].indirect(ql[:, c]), T.mk[:], OP.mult)
+            sd = vec([sg, t_rs], V.tensor_tensor_scan, T.SD[:, w], T.rs[:], T.FG[:, w], 0.0, OP.mult, OP.add)
+            z1 = tt([sd, f_b], T.r1[:, c], T.SD[:, 512 * h + 15:512 * h + 512:16], T.qf[:, c], OP.subtract)
+            z2 = ts([z1], T.r2[:, c], T.r1[:, c], 15, None, OP.bitwise_and)
+            z3 = ts([z2], T.r3[:, c], T.r2[:, c], 0.0, 0.0625, OP.is_equal, OP.mult)
+            z4 = tt([z3], T.r4[:, c], T.r1[:, c], T.r3[:, c], OP.mult)
+            z5 = tt([z4], T.r5[:, o], T.r4[:, 32 * h:32 * h + 16], T.r4[:, 32 * h + 16:32 * h + 32], OP.max)
+            z6 = ts([z5], T.r6[:, o], T.r5[:, o], 1023, None, OP.bitwise_and)
+            z7 = vec([z6], V.tensor_copy, B("lo")[:, o], T.r6[:, o])
+            remote([z7], prv, B("li")[:, o], B("lo")[:, o], "gotl%d%d" % (t, h))
+        if t == 0:
+            late["vq"] = vec([d_v], V.quantize_mx, T.vq[:], T.vs[:], T.vin[:])
         got_c = ("gotc%d" % t, 2 * ein[nxt])
         for b in range(4):
             D = mm([t_P[b], late["ke"], got_c], T.psR[:, 512 * b:512 * b + 512], T.eq[:, 128 * b:128 * b + 128], T.es[:, 128 * b:128 * b + 128], B("lc")[:], B("ls")[:])
             free["psR"] = act([D, late["dz"]], T.dw[:, 528 * b + 1:528 * b + 513], T.psR[:, 512 * b:512 * b + 512])
         X = T["X%d" % (t + 1)]
-        got_l = ("gotl%d" % t, ein[nxt])
-        for b in range(4):
-            xn = tt([got_l, free["psR"]], X[:, b:2048:4], T.dw[:, 528 * b:528 * b + 513].indirect(B("li")[:]), P[:, b:2048:4], OP.add)
         xq, xs = T["xq_%d" % (t + 1)], T["xs_%d" % (t + 1)]
-        t_qx = vec([xn], V.quantize_mx, xq[:], xs[:], X[:])
+        t_qx = []
+        for h in range(2):
+            got_l = ("gotl%d%d" % (t, h), ein[nxt])
+            for b in range(4):
+                xn = tt([got_l, free["psR"]], X[:, 1024 * h + b:1024 * h + 1024:4], T.dw[:, 528 * b:528 * b + 513].indirect(B("li")[:, 16 * h:16 * h + 16]),
+                        P[:, 1024 * h + b:1024 * h + 1024:4], OP.add)
+                if t + 1 < ROUNDS and h == 1 and b == 2:
+                    addresses(0)
+            t_qx.append(vec([xn], V.quantize_mx, xq[:, half[h]], xs[:, half[h]], X[:, 1024 * h:1024 * h + 1024]))
+            if t + 1 < ROUNDS:
+                signs(t + 1, h, t_qx[h])
 
-    need("y", [t_qx])
-    g.sync.dma_start(T.oc[:], xq[:].bitcast(dt.uint8)).then_inc(T.sem.stc, 16)
-    need("a", [t_qx])
+    ym = [mm([t_qx[h], late["vq"], free["psS"], free["psM"]], half_bank[h][:, 0:256], T.vq[:], T.vs[:], xq[:, half[h]], xs[:, half[h]]) for h in range(2)]
+    dma("y", "stc0", T.oc[:, 0:1024], xq[:, 0:256].bitcast(dt.uint8), [t_qx[0]])
+    y0 = act([ym[0]], T.yo[:, 0:256], T.psS[:, 0:256])
+    dma("a", "sty0", T.y[:, 0:256], T.yo[:, 0:256], [y0])
+    dma("y", "stc1", T.oc[:, 1024:2048], xq[:, 256:512].bitcast(dt.uint8), [t_qx[1]])
+    need("a", [t_qx[1]])
     for j in range(4):
         S.dma_start(T.osc[4 * j:4 * j + 4, :], xs[32 * j:32 * j + 4, :]).then_inc(T.sem.sts, 16)
-    ym = mm([t_qx, late["vq"], free["psS"]], T.psS[:], T.vq[:], T.vs[:], xq[:], xs[:])
-    yo = vec([ym], V.tensor_copy, T.yo[:], T.psS[:])
-    need("y", [yo])
-    g.sync.dma_start(T.y[:], T.yo[:]).then_inc(T.sem.sty, 16)
+    y1 = vec([ym[1]], V.tensor_copy, T.yo[:, 256:512], T.psM[:, 0:256])
+    dma("y", "sty1", T.y[:, 256:512], T.yo[:, 256:512], [y1])
     need("g", [(s, c) for s, c in count.items()])
     g.wait_ge(T.sem.sent, sent[0])
-    g.sync.wait_ge(T.sem.stc, 16)
-    g.sync.wait_ge(T.sem.sty, 16)
-    S.wait_ge(T.sem.sts, 64)
+    need("y", [("stc0", 16), ("stc1", 16), ("sty1", 16)])
+    need("a", [("sty0", 16), ("sts", 64)])

@@ -5,22 +5,25 @@ from concourse.mybir import dt, AluOpType as OP, ActivationFunctionType as AF
 F32, F16, BF, I32, U16, U8, MX = "float32", "float16", "bfloat16", "int32", "uint16", "uint8", "float8_e4m3fn_x4"
 ROUNDS = 2
 LN2 = float(np.log(2.0))
+RUN, PLACE, PRINT, EMPTY = 0, 1, 3, 16
+W_RUN, W_PLACE, W_PRINT = 32.0, 1.0, 4096.0
+BIG = 2.0 ** 18
+ORDER = [0] * 5 + [0, 1] * 2 + [1] * 5
 SCRATCH = {"psR": ("psum", [128, 2048], F32), "psS": ("psum", [128, 512], F32), "psM": ("psum", [128, 512], F32), "psA": ("psum", [128, 1024], F32)}
 for _d, _s in [
-    (BF, "xin 2048 X1 2048 X2 2048 uin 512 vin 512 P 2048 dw 2112 ones 512 me 64 m0 128 cc 4096 ce 2048 mk 512 rs 512 bu 2048 bq 512 EA 512 EB 512 GG 512 EE 512"),
-    (MX, "uq 128 vq 128 wq 512 kq 1024 eq 512 xq_0 512 xq_1 512 xq_2 512 buq 512 bqq 128 eqa 128 eqb 128 pq_0 512 pq_1 512 lc_0 512 lc_1 512 gq 128 nq 128"),
-    (U8, "us 128 vs 128 wsc 512 ks 1024 es 512 xs_0 512 xs_1 512 xs_2 512 bus 512 bqs 128 esa 128 esb 128 psc_0 512 psc_1 512 ls_0 512 ls_1 512 gsc 128 nsc 128"),
+    (BF, "xin 2048 X1 2048 X2 2048 uin 512 vin 512 P 2048 dw 2112 ones 512 me 64 m3 64 m0 128 cc 4096 ce 2048 bu 2048 bq 512 EA 512 EB 512 GG 512 EE 512 FG 1024"),
+    (MX, "uq 128 vq 128 wq 512 kq 1024 eq 512 xq_0 512 xq_1 512 xq_2 512 buq 512 bqq 128 eqa 128 eqb 128 pq_0 512 pq_1 512 lc_0 512 lc_1 512 gq 128 nq 128 fq 256"),
+    (U8, "us 128 vs 128 wsc 512 ks 1024 es 512 xs_0 512 xs_1 512 xs_2 512 bus 512 bqs 128 esa 128 esb 128 psc_0 512 psc_1 512 ls_0 512 ls_1 512 gsc 128 nsc 128 fs 256"),
     (F16, "AA 512 AB 512 TA 512 TB 512"),
-    (F32, "yo 512 pF 5 iot 512 w4 128 g8 8 gg 8 gp 8 gm 8 wx 1 wxh 1 tw 4 w8a 8 w8n 8 ba 8 ba0 8 ba1 8 mk4 128 mp 512 idc 512 cs8 512 dc 4 "
-          "e1 128 e2 64 aw 32 h1 128 h2 64 vv 512 y1 128 y2 64 yw 32 tab_0 1056 tab_1 1056 "
-          "FG 1024 SD 1024 g1 128 g2 64 gw 32 s5 32 s6 32 qf 64 r3 64 r4 64 hq_0 32 hq_1 32 qh_0 32 qh_1 32"),
-    (I32, "pI 1 pK 5 i1 32 i2 32 r1 64 r2 64 r5 32 r6 32"),
+    (F32, "yo 512 pF 5 iot 512 w4 128 g8 8 gg 8 gp 8 gm 8 col 9 wd 4 tw 4 w8a 8 w8w 8 w8n 8 w8s 8 w8g 8 ba 8 ba0 8 ba1 8 keep 128 kept 256 mp 512 idc 512 run 512 dc 4 "
+          "vv 512 sy 128 sz 128 sn 256 tab_0 1056 tab_1 1056 s5 32 s6 32 r2 64 r3 64 r4 64"),
+    (I32, "pI 1 pK 5 nn 64 ii 64 r5 32 r6 32 hq_0 32 hq_1 32 qh_0 32 qh_1 32"),
     (U16, "la_0 64 la_1 64 of1 32 of2 32 ql_0 64 ql_1 64 lo_0 32 lo_1 32 li_0 32 li_1 32"),
 ]:
     _s = _s.split()
     for _i in range(0, len(_s), 2):
         SCRATCH[_s[_i]] = ("sbuf", [128, int(_s[_i + 1])], _d)
-SEMAPHORES = ["sv", "sa", "sp", "sg", "ldx0", "ldx1", "ldu", "ldv", "ldw", "ldws", "sty0", "sty1", "stc0", "stc1", "sts", "sent",
+SEMAPHORES = ["sv", "sa", "sp", "sg", "ldx0", "ldx1", "ldu", "ldv", "ldw", "ldws", "ldi0", "ldi1", "sty0", "sty1", "stc0", "stc1", "sts", "sent",
               "gotq0", "gotq1", "gotc0", "gotc1", "gotl00", "gotl01", "gotl10", "gotl11"]
 
 
@@ -106,12 +109,12 @@ def rank_program(g, core, T, topo):
     t_gp = iota(T.gp[:], [[0, 4], [1, 2]])
     t_m0 = select([t_ones], T.m0[:], T.ones[:, 0:128], [[0, 32], [1, 4]], OP.is_equal)
     t_me = select([], T.me[:], T.ones[:, 0:64], [[0, 4], [1, 4], [-1, 4]], OP.is_equal)
+    t_m3 = select([], T.m3[:], T.ones[:, 0:64], [[1, 64]], OP.is_equal, -4 * PRINT)
+    t_iot = iota(T.iot[:], [[0, 16], [1, 32]], -16)
     t_w4 = iota(T.w4[:], [[0, 32], [1, 4]])
-    t_iot = iota(T.iot[:], [[0, 16], [1, 32]])
-    tabs = [iota(T.tab_0[:, 0:1024], [[0, 1024]], 5)]
-    t_idc = iota(T.idc[:], [[16, 512]], 16)
-    t_cs8 = iota(T.cs8[:], [[512, 16], [0, 32]], 12)
-    t_rs = select([], T.rs[:], T.ones[:], [[0, 32], [1, 16]], OP.not_equal)
+    t_run = iota(T.run[:], [[1, 16], [0, 32]])
+    t_z = iota(T.idc[:], [[0, 512]])
+    tabs = [iota(T.tab_0[:, 0:1024], [[0, 1024]], EMPTY)]
 
     def unpackers():
         for b in range(4):
@@ -121,19 +124,32 @@ def rank_program(g, core, T, topo):
     for j, (sh, am) in enumerate([(0, 15), (0, 31), (4, 7), (2, 3), (5, 3)]):
         t_k = ts([t_pI], T.pK[:, j:j + 1], T.pI[:], sh, am, OP.logical_shift_right, OP.bitwise_and)
     t_pF = vec([t_k], V.tensor_copy, T.pF[:], T.pK[:])
-    t_wb = act([t_pF, t_b], T.wx[:], T.pF[:, 0:1], AF.Exp, bias=T.tw[:, 3:4], scale=LN2)
+    act([t_ones], T.bu[:, 0:512], T.ones[:], scale=0.0)
+    t_wb = act([t_pF, t_b], T.col[:, 0:1], T.pF[:, 0:1], AF.Exp, bias=T.tw[:, 3:4], scale=LN2)
+    for j in range(1, 4):
+        t_bu = act([], T.bu[:, 512 * j:512 * j + 512], T.ones[:], scale=0.0)
     t_gm = ts([t_pF, t_g8], T.gm[:], T.g8[:], T.pF[:, 2:3], None, OP.is_equal)
     t1 = ts([], T.tw[:, 0:1], T.pF[:, 0:1], 10.0, -1.0, OP.is_lt, OP.mult)
     t2 = ts([], T.tw[:, 1:2], T.pF[:, 0:1], 10.0, None, OP.is_ge)
     t3 = ts([], T.tw[:, 2:3], T.pF[:, 0:1], 12.0, None, OP.is_lt)
+    for j, (row, w) in enumerate([(RUN, -2048.0), (RUN, W_RUN), (PLACE, W_PLACE), (PRINT, W_PRINT)]):
+        t_wd = ts([], T.wd[:, j:j + 1], T.pF[:, 0:1], float(row), w, OP.is_equal, OP.mult)
     t_ba = ts([t_gp], T.ba[:], T.gg[:], T.pF[:, 4:5], 2048.0, OP.is_equal, OP.mult)
-    t_bu = vec([], V.memset, T.bu[:], 0.0)
+    t_r16 = ts([], T.col[:, 4:5], T.pF[:, 1:2], -16.0, None, OP.add)
+    t_end = ts([], T.col[:, 6:7], T.pF[:, 3:4], -4.0, BIG, OP.add, OP.mult)
     t_ba1 = tt([t_ba], T.ba1[:], T.ba[:], T.gp[:], OP.mult)
+    for look in range(2):
+        ts([t_end], T.col[:, 7 + look:8 + look], T.col[:, 6:7], 3.0 * W_PRINT + 17.0 + 1024.0 * (1 - look), None, OP.add)
+    t_ws = ts([t_wd], T.col[:, 5:6], T.wd[:, 1:2], T.wd[:, 2:3], T.wd[:, 3:4], OP.add, OP.add)
+    t_w8g = ts([t_gm], T.w8g[:], T.gm[:], T.wd[:, 0:1], None, OP.mult)
     t_ba0 = tt([t_ba1], T.ba0[:], T.ba[:], T.ba1[:], OP.subtract)
-    t_w8 = ts([t_wb, t1, t_gm], T.w8a[:], T.gm[:], T.wx[:, 0:1], T.tw[:, 0:1], OP.mult, OP.mult)
-    t4 = ts([t3], T.wxh[:], T.tw[:, 1:2], T.tw[:, 2:3], T.wx[:, 0:1], OP.mult, OP.mult)
-    t_w8n = ts([t4], T.w8n[:], T.gm[:], T.wxh[:, 0:1], -1.0 / 512.0, OP.mult, OP.mult)
-    t_gm2 = ts([t_ba0], T.ba[:], T.gm[:], -128.0, None, OP.mult)
+    t_w8s = ts([t_ws], T.w8s[:], T.gm[:], T.col[:, 5:6], None, OP.mult)
+    t5 = ts([t_wb, t1], T.col[:, 1:2], T.col[:, 0:1], T.tw[:, 0:1], None, OP.mult)
+    t4 = ts([t3], T.col[:, 2:3], T.tw[:, 1:2], T.tw[:, 2:3], T.col[:, 0:1], OP.mult, OP.mult)
+    t_w8 = ts([t5], T.w8a[:], T.gm[:], T.col[:, 1:2], None, OP.mult)
+    t6 = ts([t4], T.col[:, 3:4], T.col[:, 2:3], -2.0 ** -13, T.col[:, 1:2], OP.mult, OP.add)
+    t_w8n = ts([t4], T.w8n[:], T.gm[:], T.col[:, 2:3], -1.0 / 512.0, OP.mult, OP.mult)
+    t_w8w = ts([t6], T.w8w[:], T.gm[:], T.col[:, 3:4], None, OP.mult)
     for a in range(4):
         for par in range(2):
             c = 512 * par + 128 * a
@@ -144,37 +160,36 @@ def rank_program(g, core, T, topo):
             t_f = act(deps, T.cc[:, first + 64 * q:first + 64 * q + 64], src[:, 0:64], scale=col[:, q:q + 1])
         return t_f
 
-    t_cW = fill(1024, T.me, T.w8a, [t_w8, t_me])
-    t_cF = fill(1536, T.m0, T.w8n, [t_w8n, t_m0])
-    for first, src in ((2048, T.ba0), (2560, T.ba1)):
-        for q in range(8):
-            t_cR = ts([t_ba0, t_me], T.cc[:, first + 64 * q:first + 64 * q + 64], T.me[:], src[:, q:q + 1], None, OP.mult)
+    t_cW = fill(1024, T.me, T.w8w, [t_w8w, t_me])
+    fill(1536, T.m3, T.w8n, [t_w8n, t_m3])
+    t_dig = [dma("y", "ldi%d" % j, T.idc[row:128:16, :], src[row:128:16, :], [t_z, t_run]) for j, (row, src) in enumerate(((RUN, T.run), (PLACE, T.iot)))]
     vec([d_u], V.quantize_mx, T.uq[:], T.us[:], T.uin[:])
     t_qx = [vec([d_x[h]], V.quantize_mx, T.xq_0[:, 256 * h:256 * h + 256], T.xs_0[:, 256 * h:256 * h + 256], T.xin[:, 1024 * h:1024 * h + 1024]) for h in range(2)]
 
     def constants_1():
         late["kA"] = vec([t_cA, t_cW], V.quantize_mx, T.kq[:, 0:384], T.ks[:, 0:384], T.cc[:, 0:1536])
-        late["mk4"] = ts([t_w4], T.mk4[:], T.w4[:], T.pF[:, 3:4], None, OP.is_equal)
-        late["mk0"] = ts([t_iot], T.mk[:, 0:16], T.iot[:, 0:16], T.pF[:, 0:1], None, OP.is_equal)
+        late["m"] = ts([t_w4], T.keep[:], T.w4[:], T.pF[:, 3:4], 5.0 * BIG, OP.is_ge, OP.mult)
+
+    def constants_2():
+        late["mp"] = ts([t_iot, t_r16], T.mp[:], T.iot[:], T.col[:, 4:5], 4096.0, OP.is_ge, OP.mult)
+        m = ts([late["m"]], T.keep[:], T.keep[:], -4.0 * BIG, None, OP.add)
+        late["keep"] = ts([m, t_end], T.keep[:, 3::4], T.w4[:, 3::4], 0.0, T.col[:, 6:7], OP.mult, OP.add)
 
     def constants_3():
-        fill(3072, T.me, T.w8n, [])
-        late["cG"] = fill(3584, T.me, T.ba, [t_gm2])
-        for j, base in enumerate((512.5, 513.5, 1024.0, 1025.0)):
+        fill(2048, T.me, T.ba0, [t_ba0])
+        late["cR"] = fill(2560, T.me, T.ba1, [])
+        for j, base in enumerate((512.3125 - BIG, 513.3125 - BIG, 1024.0, 1025.0)):
             late["dc"] = act([], T.dc[:, j:j + 1], T.pF[:, 0:1], AF.Copy, scale=2.0, bias=base)
 
-    def masks(t):
-        w = 16
-        while w < 512:
-            t = act([t], T.mk[:, w:2 * w], T.mk[:, 0:w])
-            w *= 2
-        late["mk"] = t
+    def constants_4():
+        fill(3072, T.me, T.w8s, [t_w8s])
+        late["cS"] = fill(3584, T.me, T.w8g, [t_w8g])
 
     def k(i):
         return T.kq[:, 128 * i:128 * i + 128], T.ks[:, 128 * i:128 * i + 128]
 
-    def lower(x):
-        return x[:, 0::2], x[:, 1::2]
+    def own_word(deps, out, bank, push):
+        return vec(deps, V.tensor_tensor_scan, out, bank, push, -4.0 * BIG, OP.max, OP.add)
 
     ein = {p: len(topo.engines(p, core)) for p in (prv, nxt)}
     free = {"psS": None, "psM": None, "psA": None, "psR": None}
@@ -219,137 +234,150 @@ def rank_program(g, core, T, topo):
             constants_3()
             constants_1()
             addresses(0)
-            late["mp"] = ts([t_iot], T.mp[:], T.iot[:], T.pF[:, 1:2], 4096.0, OP.is_ge, OP.mult)
+            constants_2()
         layer(2)
         a0, a1 = masked(0, 0), masked(1, 0)
         x0, x1 = turned(0, 0, a0), turned(1, 0, a1)
         addresses(1)
         e00 = equal(0, 0, x0)
         q_bq = vec([st["bq"]], V.quantize_mx, T.bqq[:], T.bqs[:], T.bq[:])
-        if t == 0:
-            late["kR"] = vec([t_cF, t_cR], V.quantize_mx, T.kq[:, 384:768], T.ks[:, 384:768], T.cc[:, 1536:3072])
-        WA = mm([q_bq], T.psM[:, 0:128], *k(2), T.bqq[:], T.bqs[:])
-        layer(3)
-        H = mm([late["kR"]], T.psS[:], *k(3), T.buq[:], T.bus[:])
         e10 = equal(1, 0, x1)
-        mm([e00], T.psA[:, 0:128], *k(2), T.bqq[:], T.bqs[:], True, False)
         a0, a1 = masked(0, 1), masked(1, 1)
-        x0 = turned(0, 1, a0)
-        w1 = tt([WA, late["mk4"]], T.e1[:], T.psM[:, 0:128], T.mk4[:], OP.mult)
+        if t == 0:
+            late["kR"] = vec([late["cR"]], V.quantize_mx, T.kq[:, 384:768], T.ks[:, 384:768], T.cc[:, 1536:3072])
+        layer(3)
+        mm([e00, q_bq], T.psA[:, 0:128], *k(2), T.bqq[:], T.bqs[:], True, False)
+        H = mm([late["kR"]], T.psS[:], *k(3), T.buq[:], T.bus[:])
+        x0, x1 = turned(0, 1, a0), turned(1, 1, a1)
         e01 = equal(0, 1, x0)
-        x1 = turned(1, 1, a1)
+        e11 = equal(1, 1, x1)
         q0 = vec([e01], V.quantize_mx, T.eqa[:], T.esa[:], T.EA[:])
         mm([q0], T.psA[:, 0:128], *k(4), T.eqa[:], T.esa[:], False, False)
-        e11 = equal(1, 1, x1)
-        w2 = tt([w1], T.e2[:], *lower(T.e1), OP.add)
         q1 = vec([e11], V.quantize_mx, T.eqb[:], T.esb[:], T.EB[:])
         Y = mm([q1], T.psA[:, 0:128], *k(5), T.eqb[:], T.esb[:], False, True)
-        aw = tt([w2], T.aw[:], *lower(T.e2), OP.add)
-        vv = tt([H, t_idc], T.vv[:], T.psS[:], T.idc[:], OP.add)
-        free["psS"] = vv
-        if t == 0:
-            late["kG"] = vec([late["cG"]], V.quantize_mx, T.kq[:, 768:1024], T.ks[:, 768:1024], T.cc[:, 3072:4096])
-        WH = mm([w1, late["kG"]], T.psM[:, 0:128], *k(6), T.bqq[:], T.bqs[:])
         layer(0, e01)
         layer(1, e11)
+        if t == 0:
+            constants_4()
         t_P = [None] * 4
         for b in (2, 3, 0, 1):
             t_P[b] = act([r_b[b]], P[:, b:2048:4], T.psR[:, 512 * b:512 * b + 512], scale=0.03125)
-        if t == 0:
-            masks(late["mk0"])
-        y1 = tt([Y], T.y1[:], T.psA[:, 0:128], T.mk4[:], OP.mult)
-        i1 = ts([aw], T.i1[:], T.aw[:], 512.5, None, OP.add)
-        y2 = tt([y1], T.y2[:], *lower(T.y1), OP.add)
-        i2 = ts([i1], T.i2[:], T.i1[:], 1023, None, OP.bitwise_and)
-        yw = tt([y2], T.yw[:], *lower(T.y2), OP.add)
-        l0 = ts([aw], la[:, 0:16], T.aw[:, 0:16], 511.5, None, OP.add)
+
+        def digits(c):
+            c = slice(128 * c, 128 * c + 128)
+            return tt([H, *t_dig], T.vv[:, c], T.psS[:, c], T.idc[:, c], OP.add)
+
+        vv = {3: digits(3), 2: digits(2)}
+        yw = own_word([Y, late["keep"]], T.sy[:], T.psA[:, 0:128], T.keep[:])
         for c in range(2):
-            o1 = ts([yw, late["dc"]], T.of1[:, c:32:2], T.yw[:, c:32:2], T.dc[:, c:c + 1], 511.5, OP.min, OP.add)
-        sc, hx = None, None
+            o1 = ts([yw, late["dc"]], T.of1[:, c:32:2], T.sy[:, 4 * c + 3::8], T.dc[:, c:c + 1], 511.6875 + BIG, OP.min, OP.add)
+        sc, q_P = None, []
         for j in range(16):
             b = 15 - j
-            sc = vec([tabs[t], o1, vv, sc], V.tensor_copy, tab[:, 0:1056].indirect(T.of1[:, 2 * b:2 * b + 2]), T.vv[:, 32 * b:32 * b + 32])
+            sc = vec([tabs[t], o1, vv[b // 4], sc], V.tensor_copy, tab[:, 0:1056].indirect(T.of1[:, 2 * b:2 * b + 2]), T.vv[:, 32 * b:32 * b + 32])
             if j < 2:
-                l1 = vec([i2], V.tensor_copy, la[:, 32 * j + 16:32 * j + 32], T.i2[:, 16 * j:16 * j + 16])
+                nn = ts([yw], T.nn[:, 32 * j:32 * j + 32], T.sy[:, 3::4], 8.0, 4093.5 + 8.0 * j + 8.0 * BIG, OP.mult, OP.add)
             elif j == 2:
-                l0 = ts([aw], la[:, 32:48], T.aw[:, 16:32], 511.5, None, OP.add)
+                vv[1] = digits(1)
             elif j == 3:
-                hx = free["psM"] = tt([WH], T.h1[:], T.psM[:, 0:128], T.mk4[:], OP.mult)
+                ii = ts([nn], T.ii[:], T.nn[:], 3, 1023, OP.logical_shift_right, OP.bitwise_and)
             elif j == 4:
-                hx = tt([hx], T.h2[:], *lower(T.h1), OP.add)
+                hx = ts([], hq[:], T.nn[:, 0:32], 7, None, OP.bitwise_and)
             elif j == 5:
-                hx = tt([hx], hq[:], *lower(T.h2), OP.add)
-            elif j == 9:
-                q_P = vec(t_P, V.quantize_mx, B("pq")[:], B("psc")[:], P[:])
-        need("g", [l0, l1, hx])
+                l1 = vec([ii], V.tensor_copy, la[:], T.ii[:])
+            elif j == 6:
+                vv[0] = free["psS"] = digits(0)
+            elif t == 0 and j == 7:
+                late["kG"] = vec([late["cS"]], V.quantize_mx, T.kq[:, 768:1024], T.ks[:, 768:1024], T.cc[:, 3072:4096])
+            elif 9 <= j < 13:
+                i = j - 9
+                q_P.append(vec(t_P, V.quantize_mx, B("pq")[:, 128 * i:128 * i + 128], B("psc")[:, 128 * i:128 * i + 128], P[:, 512 * i:512 * i + 512]))
+        need("g", [l1, hx])
         rid, pid = topo.addr(nxt)[:2]
         es = topo.engines(core, nxt)
         m = len(es) // 2
         g.remote_dma_fused([RemoteDMATransfer(dst_ids=[DstId(rid=rid, pnc=pid)], dma_engine_mask=bits(e), remote_sem=T.sem["gotq%d" % t], src=s, dst=d)
                             for e, s, d in ((es[:m], la[:], B("ql")[:]), (es[m:], hq[:], B("qh")[:]))], local_sem=T.sem.sent)
         sent[0] += len(es)
-        remote([q_P], prv, B("lc")[:].bitcast(dt.uint8), B("pq")[:].bitcast(dt.uint8), "gotc%d" % t)
-        remote([q_P], prv, B("ls")[:], B("psc")[:], "gotc%d" % t)
+        remote(q_P, prv, B("lc")[:].bitcast(dt.uint8), B("pq")[:].bitcast(dt.uint8), "gotc%d" % t)
+        remote(q_P, prv, B("ls")[:], B("psc")[:], "gotc%d" % t)
         if t == 0:
             unpackers()
-            tabs.append(iota(T.tab_1[:, 0:1024], [[0, 1024]], 5))
-        for h in range(2):
-            em = act([sc, l1], T.EE[:, half[h]], tab[:, 0:1024].indirect(la[:, 32 * h + 16:32 * h + 32]), AF.Sign, bias=5.5, scale=-1.0)
-        for h in range(2):
-            fe = tt([sc, l0, t_cs8], T.GG[:, half[h]], tab[:, 0:1024].indirect(la[:, 32 * h:32 * h + 16]), T.cs8[:, half[h]], OP.is_ge)
-        q_g = vec([fe], V.quantize_mx, T.gq[:], T.gsc[:], T.GG[:])
-        q_e = vec([em], V.quantize_mx, T.nq[:], T.nsc[:], T.EE[:])
+            tabs.append(iota(T.tab_1[:, 0:1024], [[0, 1024]], EMPTY))
+        em = act([sc, l1], T.EE[:], tab[:, 0:1024].indirect(la[:, 32:64]), AF.Sign, bias=0.5 - EMPTY)
+        fe = tt([sc, l1, t_run], T.GG[:], tab[:, 0:1024].indirect(la[:, 0:32]), T.run[:], OP.is_ge)
         mm([e11], T.psA[:, 512:640], *k(4), T.eqa[:], T.esa[:], True, False)
         mm([], T.psA[:, 512:640], *k(5), T.eqb[:], T.esb[:], False, False)
-        mm([q_g], T.psA[:, 512:640], *k(7), T.gq[:], T.gsc[:], False, False)
+        q_g = vec([fe], V.quantize_mx, T.gq[:], T.gsc[:], T.GG[:])
+        mm([q_g, late["kG"]], T.psA[:, 512:640], *k(7), T.gq[:], T.gsc[:], False, False)
+        q_e = vec([em], V.quantize_mx, T.nq[:], T.nsc[:], T.EE[:])
         Z = mm([q_e], T.psA[:, 512:640], *k(7), T.nq[:], T.nsc[:], False, True)
-        n1 = tt([Z], T.g1[:], T.psA[:, 512:640], T.mk4[:], OP.mult)
-        free["psA"] = n1
-        n2 = tt([n1], T.g2[:], *lower(T.g1), OP.add)
-        n3 = tt([n2], T.gw[:], *lower(T.g2), OP.add)
-        n4 = ts([n3], T.s6[:], T.gw[:], -2048.0, 2048.0, OP.not_equal, OP.mult)
-        n5 = tt([n4], T.s5[:], T.s6[:], T.i2[:], OP.add)
+        n3 = free["psA"] = own_word([Z], T.sz[:], T.psA[:, 512:640], T.keep[:])
+        n4 = ts([n3], T.s6[:], T.sz[:, 3::4], -2048.0 - BIG, 2048.0, OP.not_equal, OP.mult)
+        n5 = tt([n4], T.s5[:], T.s6[:], T.ii[:, 32:64], OP.add)
         for c in range(2):
             o2 = ts([n5], T.of2[:, c:32:2], T.s5[:, c:32:2], T.dc[:, 2 + c:3 + c], None, OP.min)
         got_q = ("gotq%d" % t, ein[prv])
         ql, qh = B("ql"), B("qh")
         sc = None
         for j in range(16):
-            b, h = 15 - j, j % 2
+            b = 15 - j
             sc = vec([o2, em, sc], V.tensor_copy, tab[:, 0:1056].indirect(T.of2[:, 2 * b:2 * b + 2]), T.vv[:, 32 * b:32 * b + 32])
-            if t == 0 and j == 9:
+            if t == 0 and j == 0:
                 late["dz"] = vec([], V.memset, T.dw[:, 0:2112:528], 0.0)
-            elif 10 <= j < 12:
-                ts([got_q], T.qf[:, 32 * h:32 * h + 16], qh[:, 16 * h:16 * h + 16], -16384.0, None, OP.add)
-            elif 12 <= j < 14:
-                f_b = vec([], V.tensor_copy, T.qf[:, 32 * h + 16:32 * h + 32], qh[:, 16 * h:16 * h + 16])
-            elif t == 0 and j == 14:
-                late["ke"] = vec([late["ce"]], V.quantize_mx, T.eq[:], T.es[:], T.ce[:])
-        for h in range(2):
-            w, c, o = slice(512 * h, 512 * h + 512), slice(32 * h, 32 * h + 32), slice(16 * h, 16 * h + 16)
-            sg = tt([sc, got_q, late["mk"]], T.FG[:, w], tab[:, 0:1024].indirect(ql[:, c]), T.mk[:], OP.mult)
-            sd = vec([sg, t_rs], V.tensor_tensor_scan, T.SD[:, w], T.rs[:], T.FG[:, w], 0.0, OP.mult, OP.add)
-            z1 = tt([sd, f_b], T.r1[:, c], T.SD[:, 512 * h + 15:512 * h + 512:16], T.qf[:, c], OP.subtract)
-            z2 = ts([z1], T.r2[:, c], T.r1[:, c], 15, None, OP.bitwise_and)
-            z3 = ts([z2], T.r3[:, c], T.r2[:, c], 0.0, 0.0625, OP.is_equal, OP.mult)
-            z4 = tt([z3], T.r4[:, c], T.r1[:, c], T.r3[:, c], OP.mult)
-            z5 = tt([z4], T.r5[:, o], T.r4[:, 32 * h:32 * h + 16], T.r4[:, 32 * h + 16:32 * h + 32], OP.max)
-            z6 = ts([z5], T.r6[:, o], T.r5[:, o], 1023, None, OP.bitwise_and)
-            z7 = vec([z6], V.tensor_copy, B("lo")[:, o], T.r6[:, o])
-            remote([z7], prv, B("li")[:, o], B("lo")[:, o], "gotl%d%d" % (t, h))
-        if t == 0:
-            late["vq"] = vec([d_v], V.quantize_mx, T.vq[:], T.vs[:], T.vin[:])
+            elif t == 0 and j < 3:
+                late["kept"] = vec([late["keep"]], V.tensor_copy, T.kept[:, 128 * j - 128:128 * j], T.keep[:])
+            elif t == 0 and j == 3:
+                late["vq"] = vec([d_v], V.quantize_mx, T.vq[:], T.vs[:], T.vin[:])
+            elif 6 <= j < 10:
+                i, h, look = j - 6, (j - 6) // 2, j % 2
+                f_b = ts([got_q, late["kept"]], T.kept[:, 64 * i + 3:64 * i + 64:4], qh[:, 16 * h:16 * h + 16], -2.0 * W_PRINT, T.col[:, 7 + look:8 + look], OP.mult, OP.add)
+            elif t == 0 and 10 <= j < 14:
+                i = j - 10
+                late["ke"] = vec([late["ce"]], V.quantize_mx, T.eq[:, 128 * i:128 * i + 128], T.es[:, 128 * i:128 * i + 128], T.ce[:, 512 * i:512 * i + 512])
+        win = tab[:, 0:1024]
+        f0 = vec([sc, got_q], V.tensor_copy, T.FG[:, 0:256], win.indirect(ql[:, 0:16]))
+        f1 = act([sc, got_q], T.FG[:, 256:512], win.indirect(ql[:, 32:48]))
+        act([], T.FG[:, 512:768], win.indirect(ql[:, 16:32]))
+        f2 = act([], T.FG[:, 768:1024], win.indirect(ql[:, 48:64]))
+
+        def search(h, deps):
+            w, y, c, o = (slice(m * h, m * h + m) for m in (512, 128, 32, 16))
+            q = vec(deps, V.quantize_mx, T.fq[:, y], T.fs[:, y], T.FG[:, w])
+            N = mm([q], half_bank[h][:, 0:128], *k(6), T.fq[:, y], T.fs[:, y])
+            yield
+            z = free[("psS", "psM")[h]] = own_word([N, f_b], T.sn[:, y], half_bank[h][:, 0:128], T.kept[:, y])
+            yield
+            r = T.sn[:, 128 * h + 3:128 * h + 128:4]
+            ts([z], T.r2[:, c], r, 3000.0 - BIG, None, OP.is_le)
+            z = ts([], T.r3[:, c], r, -BIG, BIG, OP.max, OP.add)
+            yield
+            z = tt([z], T.r4[:, c], T.r2[:, c], T.r3[:, c], OP.mult)
+            yield
+            z = tt([z], T.r5[:, o], T.r4[:, 32 * h:32 * h + 16], T.r4[:, 32 * h + 16:32 * h + 32], OP.max)
+            yield
+            z = ts([z], T.r6[:, o], T.r5[:, o], 1023, None, OP.bitwise_and)
+            yield
+            z = vec([z], V.tensor_copy, B("lo")[:, o], T.r6[:, o])
+            remote([z], prv, B("li")[:, o], B("lo")[:, o], "gotl%d%d" % (t, h))
+            yield
+
+        both = [search(0, [f0, f1]), search(1, [f2])]
+        for s in ORDER:
+            next(both[s])
         got_c = ("gotc%d" % t, 2 * ein[nxt])
+        w_b = []
         for b in range(4):
             D = mm([t_P[b], late["ke"], got_c], T.psR[:, 512 * b:512 * b + 512], T.eq[:, 128 * b:128 * b + 128], T.es[:, 128 * b:128 * b + 128], B("lc")[:], B("ls")[:])
-            free["psR"] = act([D, late["dz"]], T.dw[:, 528 * b + 1:528 * b + 513], T.psR[:, 512 * b:512 * b + 512])
+            w_b.append(act([D, late["dz"]], T.dw[:, 528 * b + 1:528 * b + 513], T.psR[:, 512 * b:512 * b + 512]))
+        free["psR"] = w_b[3]
         X = T["X%d" % (t + 1)]
         xq, xs = T["xq_%d" % (t + 1)], T["xs_%d" % (t + 1)]
         t_qx = []
         for h in range(2):
             got_l = ("gotl%d%d" % (t, h), ein[nxt])
             for b in range(4):
-                xn = tt([got_l, free["psR"]], X[:, 1024 * h + b:1024 * h + 1024:4], T.dw[:, 528 * b:528 * b + 513].indirect(B("li")[:, 16 * h:16 * h + 16]),
+                xn = tt([got_l, w_b[b]], X[:, 1024 * h + b:1024 * h + 1024:4], T.dw[:, 528 * b:528 * b + 513].indirect(B("li")[:, 16 * h:16 * h + 16]),
                         P[:, 1024 * h + b:1024 * h + 1024:4], OP.add)
                 if t + 1 < ROUNDS and h == 1 and b == 2:
                     addresses(0)

@@ -11,13 +11,13 @@ BIG = 2.0 ** 18
 ORDER = [0] * 5 + [0, 1] * 2 + [1] * 5
 SCRATCH = {"psR": ("psum", [128, 2048], F32), "psS": ("psum", [128, 512], F32), "psM": ("psum", [128, 512], F32), "psA": ("psum", [128, 1024], F32)}
 for _d, _s in [
-    (BF, "xin 2048 X1 2048 X2 2048 uin 512 vin 512 P 2048 dw 2112 ones 512 me 64 m3 64 m0 128 cc 4096 ce 2048 bu 2048 bq 512 EA 512 EB 512 GG 512 EE 512 FG 1024"),
-    (MX, "uq 128 vq 128 wq 512 kq 1024 eq 512 xq_0 512 xq_1 512 xq_2 512 buq 512 bqq 128 eqa 128 eqb 128 pq_0 512 pq_1 512 lc_0 512 lc_1 512 gq 128 nq 128 fq 256"),
-    (U8, "us 128 vs 128 wsc 512 ks 1024 es 512 xs_0 512 xs_1 512 xs_2 512 bus 512 bqs 128 esa 128 esb 128 psc_0 512 psc_1 512 ls_0 512 ls_1 512 gsc 128 nsc 128 fs 256"),
+    (BF, "xin 2048 X1 2048 X2 2048 uin 512 vin 512 P 2048 dw 2112 ones 512 me 64 m3 64 m0 128 cc 4096 ce 2048 bu 2048 bq 512 EA 1024 EB 1024 GG 512 EE 512 FG 1024"),
+    (MX, "uq 128 vq 128 wq 512 kq 1024 eq 512 xq_0 512 xq_1 512 xq_2 512 buq 512 bqq 128 eqa 256 eqb 256 pq_0 512 pq_1 512 lc_0 512 lc_1 512 gq 128 nq 128 fq 256"),
+    (U8, "us 128 vs 128 wsc 512 ks 1024 es 512 xs_0 512 xs_1 512 xs_2 512 bus 512 bqs 128 esa 256 esb 256 psc_0 512 psc_1 512 ls_0 512 ls_1 512 gsc 128 nsc 128 fs 256"),
     (F16, "AA 512 AB 512 TA 512 TB 512"),
-    (F32, "yo 512 pF 5 iot 512 w4 128 g8 8 gg 8 gp 8 gm 8 col 9 wd 4 tw 4 w8a 8 w8w 8 w8n 8 w8s 8 w8g 8 ba 8 ba0 8 ba1 8 keep 128 kept 256 mp 512 idc 512 run 512 dc 4 "
-          "vv 512 sy 128 sz 128 sn 256 tab_0 1056 tab_1 1056 s5 32 s6 32 r2 64 r3 64 r4 64"),
-    (I32, "pI 1 pK 5 nn 64 ii 64 r5 32 r6 32 hq_0 32 hq_1 32 qh_0 32 qh_1 32"),
+    (F32, "yo 512 pF 6 iot 512 w4 128 g8 8 gg 8 gp 8 gm 8 col 11 wd 4 tw 4 w8a 8 w8w 8 w8n 8 w8s 8 w8g 8 ba 8 ba0 8 ba1 8 keep 128 kept 256 mp 256 idc 512 run 512 "
+          "from64 512 dc 8 vv 512 sy 128 sz 128 sn 256 tab_0 1088 tab_1 1088 s5 32 s6 32 r2 64 r3 64 r4 64"),
+    (I32, "pI 1 pK 6 nn 64 ii 64 r5 32 r6 32 hq_0 32 hq_1 32 qh_0 32 qh_1 32"),
     (U16, "la_0 64 la_1 64 of1 32 of2 32 ql_0 64 ql_1 64 lo_0 32 lo_1 32 li_0 32 li_1 32"),
 ]:
     _s = _s.split()
@@ -115,13 +115,14 @@ def rank_program(g, core, T, topo):
     t_run = iota(T.run[:], [[1, 16], [0, 32]])
     t_z = iota(T.idc[:], [[0, 512]])
     tabs = [iota(T.tab_0[:, 0:1024], [[0, 1024]], EMPTY)]
+    t_f64 = iota(T.from64[:], [[2, 8], [0, 64]])
 
     def unpackers():
         for b in range(4):
             late["ce"] = select([], T.ce[:, 512 * b:512 * b + 512], T.ones[:], [[-1, 512]], OP.is_equal, b, 4)
 
     t_b = vec([], V.memset, T.tw[:, 3:4], -LN2)
-    for j, (sh, am) in enumerate([(0, 15), (0, 31), (4, 7), (2, 3), (5, 3)]):
+    for j, (sh, am) in enumerate([(0, 15), (0, 31), (4, 7), (2, 3), (5, 3), (0, 1)]):
         t_k = ts([t_pI], T.pK[:, j:j + 1], T.pI[:], sh, am, OP.logical_shift_right, OP.bitwise_and)
     t_pF = vec([t_k], V.tensor_copy, T.pF[:], T.pK[:])
     act([t_ones], T.bu[:, 0:512], T.ones[:], scale=0.0)
@@ -137,9 +138,11 @@ def rank_program(g, core, T, topo):
     t_ba = ts([t_gp], T.ba[:], T.gg[:], T.pF[:, 4:5], 2048.0, OP.is_equal, OP.mult)
     t_r16 = ts([], T.col[:, 4:5], T.pF[:, 1:2], -16.0, None, OP.add)
     t_end = ts([], T.col[:, 6:7], T.pF[:, 3:4], -4.0, BIG, OP.add, OP.mult)
+    t_odd = ts([], T.col[:, 9:10], T.pF[:, 5:6], -1.0, 2048.0, OP.add, OP.mult)
     t_ba1 = tt([t_ba], T.ba1[:], T.ba[:], T.gp[:], OP.mult)
     for look in range(2):
         ts([t_end], T.col[:, 7 + look:8 + look], T.col[:, 6:7], 3.0 * W_PRINT + 17.0 + 1024.0 * (1 - look), None, OP.add)
+    t_end2 = ts([t_odd, t_end], T.col[:, 10:11], T.col[:, 9:10], T.col[:, 6:7], None, OP.add)
     t_ws = ts([t_wd], T.col[:, 5:6], T.wd[:, 1:2], T.wd[:, 2:3], T.wd[:, 3:4], OP.add, OP.add)
     t_w8g = ts([t_gm], T.w8g[:], T.gm[:], T.wd[:, 0:1], None, OP.mult)
     t_ba0 = tt([t_ba1], T.ba0[:], T.ba[:], T.ba1[:], OP.subtract)
@@ -171,15 +174,16 @@ def rank_program(g, core, T, topo):
         late["m"] = ts([t_w4], T.keep[:], T.w4[:], T.pF[:, 3:4], 5.0 * BIG, OP.is_ge, OP.mult)
 
     def constants_2():
-        late["mp"] = ts([t_iot, t_r16], T.mp[:], T.iot[:], T.col[:, 4:5], 4096.0, OP.is_ge, OP.mult)
+        for odd, op in enumerate((OP.is_gt, OP.is_ge)):
+            late["mp"] = ts([t_iot, t_r16], T.mp[:, 128 * odd:128 * odd + 128], T.iot[:, 0:128], T.col[:, 4:5], 4096.0, op, OP.mult)
         m = ts([late["m"]], T.keep[:], T.keep[:], -4.0 * BIG, None, OP.add)
-        late["keep"] = ts([m, t_end], T.keep[:, 3::4], T.w4[:, 3::4], 0.0, T.col[:, 6:7], OP.mult, OP.add)
+        late["keep"] = ts([m, t_end2], T.keep[:, 3::4], T.w4[:, 3::4], 0.0, T.col[:, 10:11], OP.mult, OP.add)
 
     def constants_3():
         fill(2048, T.me, T.ba0, [t_ba0])
         late["cR"] = fill(2560, T.me, T.ba1, [])
-        for j, base in enumerate((512.3125 - BIG, 513.3125 - BIG, 1024.0, 1025.0)):
-            late["dc"] = act([], T.dc[:, j:j + 1], T.pF[:, 0:1], AF.Copy, scale=2.0, bias=base)
+        for j, base in enumerate([b + c for b in (512.3125 - BIG, 1024.0) for c in range(4)]):
+            late["dc"] = act([], T.dc[:, j:j + 1], T.pF[:, 0:1], AF.Copy, scale=4.0, bias=base)
 
     def constants_4():
         fill(3072, T.me, T.w8s, [t_w8s])
@@ -204,12 +208,12 @@ def rank_program(g, core, T, topo):
         st["bq"] = act([], T.bq[:, half[h]], half_bank[h][:, 0:256], AF.Sign, bias=7.7e-34)
 
     def bank(par, h):
-        return (T.psA, T.psR)[h][:, 512 * par:512 * par + 256]
+        return [(T.psA, T.psR)[h][:, 512 * par + o:512 * par + 256:2] for o in range(2)]
 
     def addresses(h):
         q = vec([st["sg", h]], V.quantize_mx, T.buq[:, half[h]], T.bus[:, half[h]], T.bu[:, 1024 * h:1024 * h + 1024])
         for par in range(2):
-            st["A", par, h] = mm([q, late["kA"], free["psA"], free["psR"]], bank(par, h), *k(par), T.buq[:, half[h]], T.bus[:, half[h]])
+            st["A", par, h] = mm([q, late["kA"], free["psA"], free["psR"]], (T.psA, T.psR)[h][:, 512 * par:512 * par + 256], *k(par), T.buq[:, half[h]], T.bus[:, half[h]])
 
     for t in range(ROUNDS):
         B = lambda name, t=t: T["%s_%d" % (name, t)]
@@ -220,13 +224,27 @@ def rank_program(g, core, T, topo):
             r_b[b] = mm([d_w, d_ws, free["psR"], dep], T.psR[:, 512 * b:512 * b + 512], T.wq[:, 128 * b:128 * b + 128], T.wsc[:, 128 * b:128 * b + 128], xq[:], xs[:])
 
         def masked(par, h):
-            return tt([st["A", par, h], late["mp"]], (T.AA, T.AB)[par][:, half[h]], bank(par, h), T.mp[:, half[h]], OP.add)
+            for o in range(2):
+                c = 256 * h + 128 * o
+                m = tt([st["A", par, h], late["mp"]], (T.AA, T.AB)[par][:, c:c + 128], bank(par, h)[o], T.mp[:, 128 * o:128 * o + 128], OP.add)
+            return m
 
         def turned(par, h, dep):
             return vec([dep], V.transpose, (T.TA, T.TB)[par][:, half[h]], (T.AA, T.AB)[par][:, half[h]])
 
         def equal(par, h, dep):
-            return tt([dep], (T.EA, T.EB)[par][:, half[h]], bank(par, h), (T.TA, T.TB)[par][:, half[h]], OP.is_equal)
+            for r in range(2):
+                for o in range(2):
+                    c = 256 * h + 128 * r
+                    e = tt([dep], (T.EA, T.EB)[par][:, 512 * r + 256 * h + o:512 * r + 256 * h + 256:2], bank(par, h)[o], (T.TA, T.TB)[par][:, c:c + 128], OP.is_equal)
+            return e
+
+        def ranks(out, deps, first, last):
+            for i, (q, s) in enumerate(((T.eqa, T.esa), (T.eqb, T.esb))):
+                for r in range(2):
+                    w = slice(128 * r, 128 * r + 128)
+                    m = mm([deps[i]], out, *k(4 + i), q[:, w], s[:, w], first and i + r == 0, last and i + r == 2)
+            return m
 
         if t == 0:
             signs(0, 0, t_qx[0])
@@ -252,9 +270,8 @@ def rank_program(g, core, T, topo):
         e01 = equal(0, 1, x0)
         e11 = equal(1, 1, x1)
         q0 = vec([e01], V.quantize_mx, T.eqa[:], T.esa[:], T.EA[:])
-        mm([q0], T.psA[:, 0:128], *k(4), T.eqa[:], T.esa[:], False, False)
         q1 = vec([e11], V.quantize_mx, T.eqb[:], T.esb[:], T.EB[:])
-        Y = mm([q1], T.psA[:, 0:128], *k(5), T.eqb[:], T.esb[:], False, True)
+        Y = ranks(T.psA[:, 0:128], (q0, q1), False, True)
         layer(0, e01)
         layer(1, e11)
         if t == 0:
@@ -269,12 +286,13 @@ def rank_program(g, core, T, topo):
 
         vv = {3: digits(3), 2: digits(2)}
         yw = own_word([Y, late["keep"]], T.sy[:], T.psA[:, 0:128], T.keep[:])
-        for c in range(2):
-            o1 = ts([yw, late["dc"]], T.of1[:, c:32:2], T.sy[:, 4 * c + 3::8], T.dc[:, c:c + 1], 511.6875 + BIG, OP.min, OP.add)
+        for c in range(4):
+            o1 = ts([yw, late["dc"]], T.of1[:, c:32:4], T.sy[:, 4 * c + 3::16], T.dc[:, c:c + 1], 511.6875 + BIG, OP.min, OP.add)
         sc, q_P = None, []
         for j in range(16):
-            b = 15 - j
-            sc = vec([tabs[t], o1, vv[b // 4], sc], V.tensor_copy, tab[:, 0:1056].indirect(T.of1[:, 2 * b:2 * b + 2]), T.vv[:, 32 * b:32 * b + 32])
+            b = 7 - j // 2
+            if j % 2 == 0:
+                sc = vec([tabs[t], o1, vv[b // 2], sc], V.tensor_copy, tab[:, 0:1088].indirect(T.of1[:, 4 * b:4 * b + 4]), T.vv[:, 64 * b:64 * b + 64])
             if j < 2:
                 nn = ts([yw], T.nn[:, 32 * j:32 * j + 32], T.sy[:, 3::4], 8.0, 4093.5 + 8.0 * j + 8.0 * BIG, OP.mult, OP.add)
             elif j == 2:
@@ -289,8 +307,8 @@ def rank_program(g, core, T, topo):
                 vv[0] = free["psS"] = digits(0)
             elif t == 0 and j == 7:
                 late["kG"] = vec([late["cS"]], V.quantize_mx, T.kq[:, 768:1024], T.ks[:, 768:1024], T.cc[:, 3072:4096])
-            elif 9 <= j < 13:
-                i = j - 9
+            elif j > 8 and j % 2:
+                i = (j - 9) // 2
                 q_P.append(vec(t_P, V.quantize_mx, B("pq")[:, 128 * i:128 * i + 128], B("psc")[:, 128 * i:128 * i + 128], P[:, 512 * i:512 * i + 512]))
         need("g", [l1, hx])
         rid, pid = topo.addr(nxt)[:2]
@@ -305,9 +323,8 @@ def rank_program(g, core, T, topo):
             unpackers()
             tabs.append(iota(T.tab_1[:, 0:1024], [[0, 1024]], EMPTY))
         em = act([sc, l1], T.EE[:], tab[:, 0:1024].indirect(la[:, 32:64]), AF.Sign, bias=0.5 - EMPTY)
-        fe = tt([sc, l1, t_run], T.GG[:], tab[:, 0:1024].indirect(la[:, 0:32]), T.run[:], OP.is_ge)
-        mm([e11], T.psA[:, 512:640], *k(4), T.eqa[:], T.esa[:], True, False)
-        mm([], T.psA[:, 512:640], *k(5), T.eqb[:], T.esb[:], False, False)
+        fe = tt([sc, l1, t_f64], T.GG[:], tab[:, 0:1024].indirect(la[:, 0:32]), T.from64[:], OP.is_ge)
+        ranks(T.psA[:, 512:640], (q1, q1), True, False)
         q_g = vec([fe], V.quantize_mx, T.gq[:], T.gsc[:], T.GG[:])
         mm([q_g, late["kG"]], T.psA[:, 512:640], *k(7), T.gq[:], T.gsc[:], False, False)
         q_e = vec([em], V.quantize_mx, T.nq[:], T.nsc[:], T.EE[:])
@@ -315,14 +332,15 @@ def rank_program(g, core, T, topo):
         n3 = free["psA"] = own_word([Z], T.sz[:], T.psA[:, 512:640], T.keep[:])
         n4 = ts([n3], T.s6[:], T.sz[:, 3::4], -2048.0 - BIG, 2048.0, OP.not_equal, OP.mult)
         n5 = tt([n4], T.s5[:], T.s6[:], T.ii[:, 32:64], OP.add)
-        for c in range(2):
-            o2 = ts([n5], T.of2[:, c:32:2], T.s5[:, c:32:2], T.dc[:, 2 + c:3 + c], None, OP.min)
+        for c in range(4):
+            o2 = ts([n5], T.of2[:, c:32:4], T.s5[:, c:32:4], T.dc[:, 4 + c:5 + c], None, OP.min)
         got_q = ("gotq%d" % t, ein[prv])
         ql, qh = B("ql"), B("qh")
         sc = None
         for j in range(16):
-            b = 15 - j
-            sc = vec([o2, em, sc], V.tensor_copy, tab[:, 0:1056].indirect(T.of2[:, 2 * b:2 * b + 2]), T.vv[:, 32 * b:32 * b + 32])
+            b = 7 - j // 2
+            if j % 2 == 0:
+                sc = vec([o2, em, sc], V.tensor_copy, tab[:, 0:1088].indirect(T.of2[:, 4 * b:4 * b + 4]), T.vv[:, 64 * b:64 * b + 64])
             if t == 0 and j == 0:
                 late["dz"] = vec([], V.memset, T.dw[:, 0:2112:528], 0.0)
             elif t == 0 and j < 3:

import numpy as np
from concourse.bass import DstId, RemoteDMATransfer
from concourse.mybir import dt, AluOpType as OP, ActivationFunctionType as AF

F32, F16, BF, I32, U16, U8, MX = "float32", "float16", "bfloat16", "int32", "uint16", "uint8", "float8_e4m3fn_x4"
ROUNDS = 2
LN2 = float(np.log(2.0))
RUN, PLACE, PRINT, EMPTY = 0, 1, 3, 16
W_RUN, W_PLACE, W_PRINT = 32.0, 1.0, 4096.0
BIG = 2.0 ** 18
ORDER = [0] * 5 + [0, 1] * 2 + [1] * 5
SCRATCH = {"psR": ("psum", [128, 2048], F32), "psS": ("psum", [128, 512], F32), "psM": ("psum", [128, 512], F32), "psA": ("psum", [128, 1024], F32)}
for _d, _s in [
    (BF, "xin 2048 X1 2048 X2 2048 uin 512 vin 512 P 2048 dw 2112 ones 512 me 64 m3 64 m0 128 cc 4096 ce 2048 bu 2048 bq 512 EA 1024 EB 1024 GG 512 EE 512 FG 1024"),
    (MX, "uq 128 vq 128 wq 512 kq 1024 eq 512 xq_0 512 xq_1 512 xq_2 512 buq 512 bqq 128 eqa 256 eqb 256 pq_0 512 pq_1 512 lc_0 512 lc_1 512 gq 128 nq 128 fq 256"),
    (U8, "us 128 vs 128 wsc 512 ks 1024 es 512 xs_0 512 xs_1 512 xs_2 512 bus 512 bqs 128 esa 256 esb 256 psc_0 512 psc_1 512 ls_0 512 ls_1 512 gsc 128 nsc 128 fs 256"),
    (F16, "AA 512 AB 512 TA 512 TB 512"),
    (F32, "yo 512 pF 6 iot 512 w4 128 g8 8 gg 8 gp 8 gm 8 col 11 wd 4 tw 4 w8a 8 w8w 8 w8n 8 w8s 8 w8g 8 ba 8 ba0 8 ba1 8 keep 128 kept 256 mp 256 idc 512 run 512 "
          "from64 512 dc 8 vv 512 sy 128 sz 128 sn 256 tab_0 1088 tab_1 1088 s5 32 s6 32 r2 64 r3 64 r4 64"),
    (I32, "pI 1 pK 6 nn 64 ii 64 r5 32 r6 32 hq_0 32 hq_1 32 qh_0 32 qh_1 32"),
    (U16, "la_0 64 la_1 64 of1 32 of2 32 ql_0 64 ql_1 64 lo_0 32 lo_1 32 li_0 32 li_1 32"),
]:
    _s = _s.split()
    for _i in range(0, len(_s), 2):
        SCRATCH[_s[_i]] = ("sbuf", [128, int(_s[_i + 1])], _d)
SEMAPHORES = ["sv", "sa", "sp", "sg", "ldx0", "ldx1", "ldu", "ldv", "ldw", "ldws", "ldi0", "ldi1", "sty0", "sty1", "stc0", "stc1", "sts", "sent",
              "gotq0", "gotq1", "gotc0", "gotc1", "gotl00", "gotl01", "gotl10", "gotl11"]


def rank_program(g, core, T, topo):
    me = T.rank_of(core)
    if me is None:
        return
    n = len(T.cores)
    nxt, prv = T.cores[(me + 1) % n], T.cores[(me - 1) % n]
    V, S, PE = g.vector, g.scalar, g.tensor
    queue = {"v": V, "a": S, "p": PE, "g": g, "y": g.sync}
    own = {"v": "sv", "a": "sa", "p": "sp", "g": "sg"}
    count = {"sv": 0, "sa": 0, "sp": 0, "sg": 0}
    seen = {q: {} for q in queue}
    sent = [0]
    late = {}

    def need(q, deps):
        for d in deps:
            if d is not None and seen[q].get(d[0], 0) < d[1]:
                queue[q].wait_ge(T.sem[d[0]], d[1])
                seen[q][d[0]] = d[1]

    def done(q, ins):
        s = own[q]
        ins.then_inc(T.sem[s], 1)
        count[s] += 1
        return (s, count[s])

    def vec(deps, fn, *a):
        need("v", deps)
        return done("v", fn(*a))

    def ts(deps, out, in0, s1, s2, *ops):
        return vec(deps, V.tensor_scalar, out, in0, s1, s2, *ops)

    def tt(deps, out, in0, in1, op):
        return vec(deps, V.tensor_tensor, out, in0, in1, op)

    def act(deps, out, in_, func=AF.Copy, **kw):
        need("a", deps)
        return done("a", S.activation(out, in_, func, **kw))

    def mm(deps, out, lq, ls, rq, rs, start=True, stop=True):
        need("p", deps)
        return done("p", PE.matmul_mx(out, lq, ls, rq, rs, start, stop))

    def iota(out, pattern, base=0, cm=0):
        return done("g", g.iota(out, pattern, base, cm, allow_small_or_imprecise_dtypes=True))

    def select(deps, out, in_, pattern, op, base=0, cm=0):
        need("g", deps)
        return done("g", g.affine_select(out, in_, pattern, op, 0.0, base, cm))

    def dma(q, sem, out, in_, deps=()):
        need(q, deps)
        queue[q].dma_start(out, in_).then_inc(T.sem[sem], 16)
        return (sem, 16)

    def bits(es):
        m = 0
        for e in es:
            m |= 1 << e
        return m

    def remote(deps, dst, out, in_, sem):
        need("g", deps)
        rid, pid = topo.addr(dst)[:2]
        g.remote_dma(out, in_, T.sem[sem], T.sem.sent, pid, rid, topo.mask(core, dst))
        sent[0] += len(topo.engines(core, dst))

    d_x = [dma("y", "ldx0", T.xin[:, 0:1024], T.x[:, 0:1024])]
    d_u = dma("a", "ldu", T.uin[:], T.u[:])
    d_x.append(dma("y", "ldx1", T.xin[:, 1024:2048], T.x[:, 1024:2048]))
    d_w = dma("y", "ldw", T.wq[:].bitcast(dt.uint8), T.wc[:])
    d_ws = dma("y", "ldws", T.wsc[:], T.ws[:])
    d_v = dma("y", "ldv", T.vin[:], T.v[:])

    t_pI = done("g", g.iota(T.pI[:], [[0, 1]], 0, 1))
    t_ones = vec([], V.memset, T.ones[:], 1.0)
    t_g8 = iota(T.g8[:], [[1, 8]])
    iota(T.gg[:], [[1, 4], [0, 2]])
    t_gp = iota(T.gp[:], [[0, 4], [1, 2]])
    t_m0 = select([t_ones], T.m0[:], T.ones[:, 0:128], [[0, 32], [1, 4]], OP.is_equal)
    t_me = select([], T.me[:], T.ones[:, 0:64], [[0, 4], [1, 4], [-1, 4]], OP.is_equal)
    t_m3 = select([], T.m3[:], T.ones[:, 0:64], [[1, 64]], OP.is_equal, -4 * PRINT)
    t_iot = iota(T.iot[:], [[0, 16], [1, 32]], -16)
    t_w4 = iota(T.w4[:], [[0, 32], [1, 4]])
    t_run = iota(T.run[:], [[1, 16], [0, 32]])
    t_z = iota(T.idc[:], [[0, 512]])
    tabs = [iota(T.tab_0[:, 0:1024], [[0, 1024]], EMPTY)]
    t_f64 = iota(T.from64[:], [[2, 8], [0, 64]])

    def unpackers():
        for b in range(4):
            late["ce"] = select([], T.ce[:, 512 * b:512 * b + 512], T.ones[:], [[-1, 512]], OP.is_equal, b, 4)

    t_b = vec([], V.memset, T.tw[:, 3:4], -LN2)
    for j, (sh, am) in enumerate([(0, 15), (0, 31), (4, 7), (2, 3), (5, 3), (0, 1)]):
        t_k = ts([t_pI], T.pK[:, j:j + 1], T.pI[:], sh, am, OP.logical_shift_right, OP.bitwise_and)
    t_pF = vec([t_k], V.tensor_copy, T.pF[:], T.pK[:])
    act([t_ones], T.bu[:, 0:512], T.ones[:], scale=0.0)
    t_wb = act([t_pF, t_b], T.col[:, 0:1], T.pF[:, 0:1], AF.Exp, bias=T.tw[:, 3:4], scale=LN2)
    for j in range(1, 4):
        t_bu = act([], T.bu[:, 512 * j:512 * j + 512], T.ones[:], scale=0.0)
    t_gm = ts([t_pF, t_g8], T.gm[:], T.g8[:], T.pF[:, 2:3], None, OP.is_equal)
    t1 = ts([], T.tw[:, 0:1], T.pF[:, 0:1], 10.0, -1.0, OP.is_lt, OP.mult)
    t2 = ts([], T.tw[:, 1:2], T.pF[:, 0:1], 10.0, None, OP.is_ge)
    t3 = ts([], T.tw[:, 2:3], T.pF[:, 0:1], 12.0, None, OP.is_lt)
    for j, (row, w) in enumerate([(RUN, -2048.0), (RUN, W_RUN), (PLACE, W_PLACE), (PRINT, W_PRINT)]):
        t_wd = ts([], T.wd[:, j:j + 1], T.pF[:, 0:1], float(row), w, OP.is_equal, OP.mult)
    t_ba = ts([t_gp], T.ba[:], T.gg[:], T.pF[:, 4:5], 2048.0, OP.is_equal, OP.mult)
    t_r16 = ts([], T.col[:, 4:5], T.pF[:, 1:2], -16.0, None, OP.add)
    t_end = ts([], T.col[:, 6:7], T.pF[:, 3:4], -4.0, BIG, OP.add, OP.mult)
    t_odd = ts([], T.col[:, 9:10], T.pF[:, 5:6], -1.0, 2048.0, OP.add, OP.mult)
    t_ba1 = tt([t_ba], T.ba1[:], T.ba[:], T.gp[:], OP.mult)
    for look in range(2):
        ts([t_end], T.col[:, 7 + look:8 + look], T.col[:, 6:7], 3.0 * W_PRINT + 17.0 + 1024.0 * (1 - look), None, OP.add)
    t_end2 = ts([t_odd, t_end], T.col[:, 10:11], T.col[:, 9:10], T.col[:, 6:7], None, OP.add)
    t_ws = ts([t_wd], T.col[:, 5:6], T.wd[:, 1:2], T.wd[:, 2:3], T.wd[:, 3:4], OP.add, OP.add)
    t_w8g = ts([t_gm], T.w8g[:], T.gm[:], T.wd[:, 0:1], None, OP.mult)
    t_ba0 = tt([t_ba1], T.ba0[:], T.ba[:], T.ba1[:], OP.subtract)
    t_w8s = ts([t_ws], T.w8s[:], T.gm[:], T.col[:, 5:6], None, OP.mult)
    t5 = ts([t_wb, t1], T.col[:, 1:2], T.col[:, 0:1], T.tw[:, 0:1], None, OP.mult)
    t4 = ts([t3], T.col[:, 2:3], T.tw[:, 1:2], T.tw[:, 2:3], T.col[:, 0:1], OP.mult, OP.mult)
    t_w8 = ts([t5], T.w8a[:], T.gm[:], T.col[:, 1:2], None, OP.mult)
    t6 = ts([t4], T.col[:, 3:4], T.col[:, 2:3], -2.0 ** -13, T.col[:, 1:2], OP.mult, OP.add)
    t_w8n = ts([t4], T.w8n[:], T.gm[:], T.col[:, 2:3], -1.0 / 512.0, OP.mult, OP.mult)
    t_w8w = ts([t6], T.w8w[:], T.gm[:], T.col[:, 3:4], None, OP.mult)
    for a in range(4):
        for par in range(2):
            c = 512 * par + 128 * a
            t_cA = ts([t_w8, t_m0], T.cc[:, c:c + 128], T.m0[:], T.w8a[:, 2 * a + par:2 * a + par + 1], None, OP.mult)

    def fill(first, src, col, deps):
        for q in range(8):
            t_f = act(deps, T.cc[:, first + 64 * q:first + 64 * q + 64], src[:, 0:64], scale=col[:, q:q + 1])
        return t_f

    t_cW = fill(1024, T.me, T.w8w, [t_w8w, t_me])
    fill(1536, T.m3, T.w8n, [t_w8n, t_m3])
    t_dig = [dma("y", "ldi%d" % j, T.idc[row:128:16, :], src[row:128:16, :], [t_z, t_run]) for j, (row, src) in enumerate(((RUN, T.run), (PLACE, T.iot)))]
    vec([d_u], V.quantize_mx, T.uq[:], T.us[:], T.uin[:])
    t_qx = [vec([d_x[h]], V.quantize_mx, T.xq_0[:, 256 * h:256 * h + 256], T.xs_0[:, 256 * h:256 * h + 256], T.xin[:, 1024 * h:1024 * h + 1024]) for h in range(2)]

    def constants_1():
        late["kA"] = vec([t_cA, t_cW], V.quantize_mx, T.kq[:, 0:384], T.ks[:, 0:384], T.cc[:, 0:1536])
        late["m"] = ts([t_w4], T.keep[:], T.w4[:], T.pF[:, 3:4], 5.0 * BIG, OP.is_ge, OP.mult)

    def constants_2():
        for odd, op in enumerate((OP.is_gt, OP.is_ge)):
            late["mp"] = ts([t_iot, t_r16], T.mp[:, 128 * odd:128 * odd + 128], T.iot[:, 0:128], T.col[:, 4:5], 4096.0, op, OP.mult)
        m = ts([late["m"]], T.keep[:], T.keep[:], -4.0 * BIG, None, OP.add)
        late["keep"] = ts([m, t_end2], T.keep[:, 3::4], T.w4[:, 3::4], 0.0, T.col[:, 10:11], OP.mult, OP.add)

    def constants_3():
        fill(2048, T.me, T.ba0, [t_ba0])
        late["cR"] = fill(2560, T.me, T.ba1, [])
        for j, base in enumerate([b + c for b in (512.3125 - BIG, 1024.0) for c in range(4)]):
            late["dc"] = act([], T.dc[:, j:j + 1], T.pF[:, 0:1], AF.Copy, scale=4.0, bias=base)

    def constants_4():
        fill(3072, T.me, T.w8s, [t_w8s])
        late["cS"] = fill(3584, T.me, T.w8g, [t_w8g])

    def k(i):
        return T.kq[:, 128 * i:128 * i + 128], T.ks[:, 128 * i:128 * i + 128]

    def own_word(deps, out, bank, push):
        return vec(deps, V.tensor_tensor_scan, out, bank, push, -4.0 * BIG, OP.max, OP.add)

    ein = {p: len(topo.engines(p, core)) for p in (prv, nxt)}
    free = {"psS": None, "psM": None, "psA": None, "psR": None}
    half_bank = (T.psS, T.psM)
    half = (slice(0, 256), slice(256, 512))
    st = {}

    def signs(t, h, dep):
        xq, xs = T["xq_%d" % t], T["xs_%d" % t]
        s = mm([dep, free["psS"], free["psM"]], half_bank[h][:, 0:256], T.uq[:], T.us[:], xq[:, half[h]], xs[:, half[h]])
        st["sg", h] = act([s, t_bu], T.bu[:, 1024 * h:1024 * h + 1024:4], half_bank[h][:, 0:256], AF.Sign, bias=7.7e-34)
        st["bq"] = act([], T.bq[:, half[h]], half_bank[h][:, 0:256], AF.Sign, bias=7.7e-34)

    def bank(par, h):
        return [(T.psA, T.psR)[h][:, 512 * par + o:512 * par + 256:2] for o in range(2)]

    def addresses(h):
        q = vec([st["sg", h]], V.quantize_mx, T.buq[:, half[h]], T.bus[:, half[h]], T.bu[:, 1024 * h:1024 * h + 1024])
        for par in range(2):
            st["A", par, h] = mm([q, late["kA"], free["psA"], free["psR"]], (T.psA, T.psR)[h][:, 512 * par:512 * par + 256], *k(par), T.buq[:, half[h]], T.bus[:, half[h]])

    for t in range(ROUNDS):
        B = lambda name, t=t: T["%s_%d" % (name, t)]
        xq, xs, P, tab, la, hq = B("xq"), B("xs"), T.P, B("tab"), B("la"), B("hq")
        r_b = [None] * 4

        def layer(b, dep=None):
            r_b[b] = mm([d_w, d_ws, free["psR"], dep], T.psR[:, 512 * b:512 * b + 512], T.wq[:, 128 * b:128 * b + 128], T.wsc[:, 128 * b:128 * b + 128], xq[:], xs[:])

        def masked(par, h):
            for o in range(2):
                c = 256 * h + 128 * o
                m = tt([st["A", par, h], late["mp"]], (T.AA, T.AB)[par][:, c:c + 128], bank(par, h)[o], T.mp[:, 128 * o:128 * o + 128], OP.add)
            return m

        def turned(par, h, dep):
            return vec([dep], V.transpose, (T.TA, T.TB)[par][:, half[h]], (T.AA, T.AB)[par][:, half[h]])

        def equal(par, h, dep):
            for r in range(2):
                for o in range(2):
                    c = 256 * h + 128 * r
                    e = tt([dep], (T.EA, T.EB)[par][:, 512 * r + 256 * h + o:512 * r + 256 * h + 256:2], bank(par, h)[o], (T.TA, T.TB)[par][:, c:c + 128], OP.is_equal)
            return e

        def ranks(out, deps, first, last):
            for i, (q, s) in enumerate(((T.eqa, T.esa), (T.eqb, T.esb))):
                for r in range(2):
                    w = slice(128 * r, 128 * r + 128)
                    m = mm([deps[i]], out, *k(4 + i), q[:, w], s[:, w], first and i + r == 0, last and i + r == 2)
            return m

        if t == 0:
            signs(0, 0, t_qx[0])
            signs(0, 1, t_qx[1])
            constants_3()
            constants_1()
            addresses(0)
            constants_2()
        layer(2)
        a0, a1 = masked(0, 0), masked(1, 0)
        x0, x1 = turned(0, 0, a0), turned(1, 0, a1)
        addresses(1)
        e00 = equal(0, 0, x0)
        q_bq = vec([st["bq"]], V.quantize_mx, T.bqq[:], T.bqs[:], T.bq[:])
        e10 = equal(1, 0, x1)
        a0, a1 = masked(0, 1), masked(1, 1)
        if t == 0:
            late["kR"] = vec([late["cR"]], V.quantize_mx, T.kq[:, 384:768], T.ks[:, 384:768], T.cc[:, 1536:3072])
        layer(3)
        mm([e00, q_bq], T.psA[:, 0:128], *k(2), T.bqq[:], T.bqs[:], True, False)
        H = mm([late["kR"]], T.psS[:], *k(3), T.buq[:], T.bus[:])
        x0, x1 = turned(0, 1, a0), turned(1, 1, a1)
        e01 = equal(0, 1, x0)
        e11 = equal(1, 1, x1)
        q0 = vec([e01], V.quantize_mx, T.eqa[:], T.esa[:], T.EA[:])
        q1 = vec([e11], V.quantize_mx, T.eqb[:], T.esb[:], T.EB[:])
        Y = ranks(T.psA[:, 0:128], (q0, q1), False, True)
        layer(0, e01)
        layer(1, e11)
        if t == 0:
            constants_4()
        t_P = [None] * 4
        for b in (2, 3, 0, 1):
            t_P[b] = act([r_b[b]], P[:, b:2048:4], T.psR[:, 512 * b:512 * b + 512], scale=0.03125)

        def digits(c):
            c = slice(128 * c, 128 * c + 128)
            return tt([H, *t_dig], T.vv[:, c], T.psS[:, c], T.idc[:, c], OP.add)

        vv = {3: digits(3), 2: digits(2)}
        yw = own_word([Y, late["keep"]], T.sy[:], T.psA[:, 0:128], T.keep[:])
        for c in range(4):
            o1 = ts([yw, late["dc"]], T.of1[:, c:32:4], T.sy[:, 4 * c + 3::16], T.dc[:, c:c + 1], 511.6875 + BIG, OP.min, OP.add)
        sc, q_P = None, []
        for j in range(16):
            b = 7 - j // 2
            if j % 2 == 0:
                sc = vec([tabs[t], o1, vv[b // 2], sc], V.tensor_copy, tab[:, 0:1088].indirect(T.of1[:, 4 * b:4 * b + 4]), T.vv[:, 64 * b:64 * b + 64])
            if j < 2:
                nn = ts([yw], T.nn[:, 32 * j:32 * j + 32], T.sy[:, 3::4], 8.0, 4093.5 + 8.0 * j + 8.0 * BIG, OP.mult, OP.add)
            elif j == 2:
                vv[1] = digits(1)
            elif j == 3:
                ii = ts([nn], T.ii[:], T.nn[:], 3, 1023, OP.logical_shift_right, OP.bitwise_and)
            elif j == 4:
                hx = ts([], hq[:], T.nn[:, 0:32], 7, None, OP.bitwise_and)
            elif j == 5:
                l1 = vec([ii], V.tensor_copy, la[:], T.ii[:])
            elif j == 6:
                vv[0] = free["psS"] = digits(0)
            elif t == 0 and j == 7:
                late["kG"] = vec([late["cS"]], V.quantize_mx, T.kq[:, 768:1024], T.ks[:, 768:1024], T.cc[:, 3072:4096])
            elif j > 8 and j % 2:
                i = (j - 9) // 2
                q_P.append(vec(t_P, V.quantize_mx, B("pq")[:, 128 * i:128 * i + 128], B("psc")[:, 128 * i:128 * i + 128], P[:, 512 * i:512 * i + 512]))
        need("g", [l1, hx])
        rid, pid = topo.addr(nxt)[:2]
        es = topo.engines(core, nxt)
        m = len(es) // 2
        g.remote_dma_fused([RemoteDMATransfer(dst_ids=[DstId(rid=rid, pnc=pid)], dma_engine_mask=bits(e), remote_sem=T.sem["gotq%d" % t], src=s, dst=d)
                            for e, s, d in ((es[:m], la[:], B("ql")[:]), (es[m:], hq[:], B("qh")[:]))], local_sem=T.sem.sent)
        sent[0] += len(es)
        remote(q_P, prv, B("lc")[:].bitcast(dt.uint8), B("pq")[:].bitcast(dt.uint8), "gotc%d" % t)
        remote(q_P, prv, B("ls")[:], B("psc")[:], "gotc%d" % t)
        if t == 0:
            unpackers()
            tabs.append(iota(T.tab_1[:, 0:1024], [[0, 1024]], EMPTY))
        em = act([sc, l1], T.EE[:], tab[:, 0:1024].indirect(la[:, 32:64]), AF.Sign, bias=0.5 - EMPTY)
        fe = tt([sc, l1, t_f64], T.GG[:], tab[:, 0:1024].indirect(la[:, 0:32]), T.from64[:], OP.is_ge)
        ranks(T.psA[:, 512:640], (q1, q1), True, False)
        q_g = vec([fe], V.quantize_mx, T.gq[:], T.gsc[:], T.GG[:])
        mm([q_g, late["kG"]], T.psA[:, 512:640], *k(7), T.gq[:], T.gsc[:], False, False)
        q_e = vec([em], V.quantize_mx, T.nq[:], T.nsc[:], T.EE[:])
        Z = mm([q_e], T.psA[:, 512:640], *k(7), T.nq[:], T.nsc[:], False, True)
        n3 = free["psA"] = own_word([Z], T.sz[:], T.psA[:, 512:640], T.keep[:])
        n4 = ts([n3], T.s6[:], T.sz[:, 3::4], -2048.0 - BIG, 2048.0, OP.not_equal, OP.mult)
        n5 = tt([n4], T.s5[:], T.s6[:], T.ii[:, 32:64], OP.add)
        for c in range(4):
            o2 = ts([n5], T.of2[:, c:32:4], T.s5[:, c:32:4], T.dc[:, 4 + c:5 + c], None, OP.min)
        got_q = ("gotq%d" % t, ein[prv])
        ql, qh = B("ql"), B("qh")
        sc = None
        for j in range(16):
            b = 7 - j // 2
            if j % 2 == 0:
                sc = vec([o2, em, sc], V.tensor_copy, tab[:, 0:1088].indirect(T.of2[:, 4 * b:4 * b + 4]), T.vv[:, 64 * b:64 * b + 64])
            if t == 0 and j == 0:
                late["dz"] = vec([], V.memset, T.dw[:, 0:2112:528], 0.0)
            elif t == 0 and j < 3:
                late["kept"] = vec([late["keep"]], V.tensor_copy, T.kept[:, 128 * j - 128:128 * j], T.keep[:])
            elif t == 0 and j == 3:
                late["vq"] = vec([d_v], V.quantize_mx, T.vq[:], T.vs[:], T.vin[:])
            elif 6 <= j < 10:
                i, h, look = j - 6, (j - 6) // 2, j % 2
                f_b = ts([got_q, late["kept"]], T.kept[:, 64 * i + 3:64 * i + 64:4], qh[:, 16 * h:16 * h + 16], -2.0 * W_PRINT, T.col[:, 7 + look:8 + look], OP.mult, OP.add)
            elif t == 0 and 10 <= j < 14:
                i = j - 10
                late["ke"] = vec([late["ce"]], V.quantize_mx, T.eq[:, 128 * i:128 * i + 128], T.es[:, 128 * i:128 * i + 128], T.ce[:, 512 * i:512 * i + 512])
        win = tab[:, 0:1024]
        f0 = vec([sc, got_q], V.tensor_copy, T.FG[:, 0:256], win.indirect(ql[:, 0:16]))
        f1 = act([sc, got_q], T.FG[:, 256:512], win.indirect(ql[:, 32:48]))
        act([], T.FG[:, 512:768], win.indirect(ql[:, 16:32]))
        f2 = act([], T.FG[:, 768:1024], win.indirect(ql[:, 48:64]))

        def search(h, deps):
            w, y, c, o = (slice(m * h, m * h + m) for m in (512, 128, 32, 16))
            q = vec(deps, V.quantize_mx, T.fq[:, y], T.fs[:, y], T.FG[:, w])
            N = mm([q], half_bank[h][:, 0:128], *k(6), T.fq[:, y], T.fs[:, y])
            yield
            z = free[("psS", "psM")[h]] = own_word([N, f_b], T.sn[:, y], half_bank[h][:, 0:128], T.kept[:, y])
            yield
            r = T.sn[:, 128 * h + 3:128 * h + 128:4]
            ts([z], T.r2[:, c], r, 3000.0 - BIG, None, OP.is_le)
            z = ts([], T.r3[:, c], r, -BIG, BIG, OP.max, OP.add)
            yield
            z = tt([z], T.r4[:, c], T.r2[:, c], T.r3[:, c], OP.mult)
            yield
            z = tt([z], T.r5[:, o], T.r4[:, 32 * h:32 * h + 16], T.r4[:, 32 * h + 16:32 * h + 32], OP.max)
            yield
            z = ts([z], T.r6[:, o], T.r5[:, o], 1023, None, OP.bitwise_and)
            yield
            z = vec([z], V.tensor_copy, B("lo")[:, o], T.r6[:, o])
            remote([z], prv, B("li")[:, o], B("lo")[:, o], "gotl%d%d" % (t, h))
            yield

        both = [search(0, [f0, f1]), search(1, [f2])]
        for s in ORDER:
            next(both[s])
        got_c = ("gotc%d" % t, 2 * ein[nxt])
        w_b = []
        for b in range(4):
            D = mm([t_P[b], late["ke"], got_c], T.psR[:, 512 * b:512 * b + 512], T.eq[:, 128 * b:128 * b + 128], T.es[:, 128 * b:128 * b + 128], B("lc")[:], B("ls")[:])
            w_b.append(act([D, late["dz"]], T.dw[:, 528 * b + 1:528 * b + 513], T.psR[:, 512 * b:512 * b + 512]))
        free["psR"] = w_b[3]
        X = T["X%d" % (t + 1)]
        xq, xs = T["xq_%d" % (t + 1)], T["xs_%d" % (t + 1)]
        t_qx = []
        for h in range(2):
            got_l = ("gotl%d%d" % (t, h), ein[nxt])
            for b in range(4):
                xn = tt([got_l, w_b[b]], X[:, 1024 * h + b:1024 * h + 1024:4], T.dw[:, 528 * b:528 * b + 513].indirect(B("li")[:, 16 * h:16 * h + 16]),
                        P[:, 1024 * h + b:1024 * h + 1024:4], OP.add)
                if t + 1 < ROUNDS and h == 1 and b == 2:
                    addresses(0)
            t_qx.append(vec([xn], V.quantize_mx, xq[:, half[h]], xs[:, half[h]], X[:, 1024 * h:1024 * h + 1024]))
            if t + 1 < ROUNDS:
                signs(t + 1, h, t_qx[h])

    ym = [mm([t_qx[h], late["vq"], free["psS"], free["psM"]], half_bank[h][:, 0:256], T.vq[:], T.vs[:], xq[:, half[h]], xs[:, half[h]]) for h in range(2)]
    dma("y", "stc0", T.oc[:, 0:1024], xq[:, 0:256].bitcast(dt.uint8), [t_qx[0]])
    y0 = act([ym[0]], T.yo[:, 0:256], T.psS[:, 0:256])
    dma("a", "sty0", T.y[:, 0:256], T.yo[:, 0:256], [y0])
    dma("y", "stc1", T.oc[:, 1024:2048], xq[:, 256:512].bitcast(dt.uint8), [t_qx[1]])
    need("a", [t_qx[1]])
    for j in range(4):
        S.dma_start(T.osc[4 * j:4 * j + 4, :], xs[32 * j:32 * j + 4, :]).then_inc(T.sem.sts, 16)
    y1 = vec([ym[1]], V.tensor_copy, T.yo[:, 256:512], T.psM[:, 0:256])
    dma("y", "sty1", T.y[:, 256:512], T.yo[:, 256:512], [y1])
    need("g", [(s, c) for s, c in count.items()])
    g.wait_ge(T.sem.sent, sent[0])
    need("y", [("stc0", 16), ("stc1", 16), ("sty1", 16)])
    need("a", [("sty0", 16), ("sts", 64)])
